import numpy as np, ml_dtypes
CORES = [16,17,18,19,32,33,34,35]
N = 8
BF = ml_dtypes.bfloat16
W, P, R, M0, M, S, RO, TH = 4096, 256, 256, 512, 1536, 3, 2, 780
def even(rng, *shape):
    return rng.integers(0, W - 1, shape)
def uneven(rng, *shape):
    return np.minimum(np.exp2(12 * rng.random(shape)).astype(np.int64) - 1, W - 2)
def edgy(rng, *shape):
    return (rng.random(shape) < 0.4) * (W - 2)
def across(t):
    y = t ^ (W // 2)
    return np.where(y == W - 1, W - 2, y)
def look(rng):
    x = rng.integers(0, 256, (16, W)); h = W // 2; m = rng.choice(np.array([0, 8, 40, 90, 120]), h)
    x[:, h:] = np.clip(x[:, :h] + rng.integers(-m, m + 1, (16, h)), 0, 255)
    return x
def rough(rng):
    return np.minimum((np.exp2(8 * rng.random((1, W))) * rng.random((16, W))).astype(np.int64), 255)
def grow(rng, tok, stem, slots, keep=0):
    k = np.arange(16)[:, None]; o = R + keep + rng.permutation(M0 - R - 2 * keep); h = len(o) // 2
    L = np.full((16, M0), W - 1); ch = np.zeros((16, M0), np.int64); F = tok(rng, 16, M0); e = np.zeros(M0, np.int64)
    levels = [np.arange(R), o[:h], o[h:h + h // 2], o[h + h // 2:]]
    for z in range(3):
        up, dn = levels[z], levels[z + 1]; n = len(dn)
        x = rng.permutation(slots)[:n] if z == 0 else rng.permutation(16 * len(up))[:n]
        p, t = up[x >> 4], x & 15; T = tok(rng, 16, n)
        if z == 0:
            T = np.where(rng.random((16, n)) < 0.8, stem[:, x], T); T[0] = x
        s = e[p]; e[dn] = np.minimum(16, s + rng.choice(np.array([1, 1, 2, 3, 5, 8, 16]), n))
        y = (T & -16) + t; T = np.where(k == s, np.where(y == W - 1, W - 17, y), T)
        F[:, dn] = np.where(k < s, F[:, p], T)
        stray = (rng.random(n) < 0.125) & (rng.random((16, n)) < 0.5) & (k != e[dn])
        L[:, dn] = np.where((k >= s) & (k < e[dn]), T, np.where(stray, tok(rng, 16, n), W - 1)); ch[t, p] = dn
        if z == 0: L[0, dn] = np.where(rng.random(n) < 0.1, tok(rng, n), L[0, dn])
    return L, ch, F
def ask(rng, tok, F):
    k = np.arange(16)[:, None]; q = F[:, rng.integers(R, M0, P)]; z = rng.integers(1, 17, P); near = q ^ (W // 2)
    q = np.where((k > 0) & (rng.random((16, P)) < 0.3) & (near != W - 1), near, q)
    y = tok(rng, 16, P); y = np.where(rng.random((16, P)) < 0.5, (y & -16) + (q & 15), y); y = np.where(y == W - 1, W - 17, y)
    return np.where((k >= z) | (rng.random(P) < 0.125), y, q)
def draw(rng, tok, shape):
    h = (M0 - R) // 2; stem = [tok(rng, 16, W) for g in range(8)]; slots = [rng.permutation(W - 1)[:h + h // 4] for g in range(8)]; d = []
    for r in range(N):
        for g in range(8):
            L, ch, F = grow(rng, tok, stem[g], slots[g]); d.append([shape(rng), L, ch, ask(rng, tok, F)])
    return d
def apart(rng):
    return 16 * rng.permutation(R)[:P] + rng.integers(0, 15, P)
def pack(d):
    a = [np.stack([x[z] for x in d]).reshape(N, 128, -1) for z in range(4)]
    return {"desc": a[0].astype(np.float32).astype(BF), "edge": a[1].astype(np.int32), "child": a[2].astype(np.int32), "req": a[3].astype(np.int32)}
def setup_inputs(rng):
    return pack(draw(rng, even, look))
def setup_inputs_spread(rng):
    return pack(draw(rng, uneven, rough))
def setup_inputs_ends(rng):
    k = np.arange(16)[:, None]; h = (M0 - R) // 2; d = []
    stem = [edgy(rng, 16, W) for g in range(8)]; slots = [2 + rng.permutation(W - 18)[:h + h // 4] for g in range(8)]
    for r in range(N):
        for g in range(8):
            L, ch, F = grow(rng, edgy, stem[g], slots[g], 1)
            x = rng.integers(0, 2, (16, W)) * 255; x[:, 0] = 0; x[:, W - 2] = 255; x[:8, W // 2] = 0; x[8:, W // 2] = 255
            q = np.where(k >= rng.integers(1, 17, P), edgy(rng, 16, P), F[:, rng.integers(R + 1, M0 - 1, P)])
            ch[0, 0] = R; ch[1, 0] = 1; ch[14, R - 1] = M0 - 1
            L[:, R] = 0; L[15, R] = W // 2; L[:, M0 - 1] = 0; L[0, M0 - 1] = W - 2
            q[:, 0] = 0; q[15, 0] = W - 2; q[0, 1] = 1
            q[:, P - 1] = 0; q[0, P - 1] = W - 2; q[15, P - 1] = W - 2
            if g % 2: q[14, P - 1] = W - 2
            d.append([x, L, ch, q])
    return pack(d)
def setup_inputs_corners(rng):
    k = np.arange(16)[:, None]; i = np.arange(P); d = draw(rng, even, look)
    for j in range(8 * N):
        x, L, ch, q = d[j]; z = j % 11; q0 = apart(rng)
        if z in (2, 3, 4, 6, 8, 9, 10):
            ch[:] = 0; L[:] = W - 1
        if z in (9, 10):
            x = np.concatenate([rng.integers(0, 100, (16, W // 2)), rng.integers(156, 256, (16, W // 2))], axis=1)
        if z == 0:
            ch[:] = 0; q[0] = rng.choice(np.array([0, 1, 15, 16, W - 17, W - 2]), P)
            L[:, 0] = np.where(k < 8, q[:, :1], W - 1)[:, 0]
        if z == 1:
            y = int(rng.choice(np.flatnonzero(ch[:, :R].T.reshape(-1)))); e = L[:, ch[y & 15, y >> 4]][:, None]
            q = np.where((rng.random(P) < 0.5) & (k > 0) & (e < W - 1), e, q); q[0] = y
        if z in (2, 3):
            q = even(rng, 16, P); q[0] = q0; u = R + i if z == 2 else q0 >> 4; ch[q0 & 15, q0 >> 4] = u; m = rng.integers(0, 5, P)
            e = np.where(((m == 1) & (k == 15)) | ((m == 2) & (k == 0)) | ((m == 3) & (k == 1)), even(rng, 16, P), q)
            L[:, u] = np.where((m == 4) & (k >= (8 if z == 2 else np.maximum(rng.integers(-5, 16, P), 0))), W - 1, e)
        if z == 4:
            nc = (M0 - R) // 4; T = even(rng, 16, nc); T[0] = rng.permutation(W - 1)[:nc]
            for m in range(4):
                u = R + 4 * np.arange(nc) + m; L[m, u] = T[m]; ch[T[m] & 15, T[0] >> 4 if m == 0 else u - 1] = u
            q = T[:, i % nc]
        if z == 5: L[:] = W - 1
        if z == 6:
            q = even(rng, 16, P); q[0] = q0; w = q0 >> 4; a = np.flatnonzero(w % 2 == 0); ch[q0[a] & 15, w[a]] = w[a] + 1
            L[:, w[a] + 1] = np.where(k < rng.integers(1, 16, len(a)), q[:, a], even(rng, 16, len(a))); q[0] = np.where(w % 4 == 3, q0 - 32, q0)
        if z == 7: q[1:] = rng.choice(np.array([0, 1, W - 3, W - 2]), (15, 1))
        if z == 8:
            nb = P // N; nc = min((M0 - R) // 17, nb); a = rng.permutation(nb)[:nc]; o = nb + rng.permutation(P - nb)[:nc]
            m = rng.integers(2, 16, nc); p = rng.integers(1, m); u = R + 17 * np.arange(nc)
            q = even(rng, 16, P); q[0] = q0; q[:, o] = np.where(k < p, q[:, a], q[:, o]); T = q[:, a]
            h = ((T[1:] * T[:-1]) >> 5) & (W - 1); h = np.concatenate([T[:1], np.where(h == W - 1, 0, h)])
            ch[T[0] & 15, T[0] >> 4] = u; L[:, u] = np.where(k < m, T, W - 1)
            for t in range(16):
                e = m + rng.integers(0, 17 - m); ch[t, u] = u + 1 + t
                L[:, u + 1 + t] = np.where((k >= m) & (k < e), np.where(rng.random((16, nc)) < 0.1, even(rng, 16, nc), h), W - 1)
        if z == 9:
            q = even(rng, 16, P); q[0] = q0; nc = P // 16; n = np.arange(nc); c = R + n; m = rng.integers(1, 8, nc)
            s = np.sort(rng.permutation(np.flatnonzero(q0 > 15))[:9 * nc].reshape(9, nc), axis=0)
            u, o, uu, oo = [q0[s[t]] >> 4 for t in (0, 2, 8, 5)]; T = q[:, s[0]]; y = q[:, s[8]]
            q[:, s[1]] = np.where(k < m, T, np.where(k == m, np.where((T ^ 1) == W - 1, 0, T ^ 1), q[:, s[1]]))
            q[0, s[2:5]] = 16 * o + (rng.integers(0, 15, nc) + 5 * np.arange(3)[:, None]) % 15
            q[0, s[5:8]] = 16 * oo + (rng.integers(0, 15, nc) + 5 * np.arange(3)[:, None]) % 15
            ch[T[0] & 15, u] = c; ch[T[m, n] & 15, c] = o; ch[y[0] & 15, uu] = oo
            L[:, c] = np.where(k < m, T, W - 1); L[:, o] = np.where(k <= m, T, across(T))
            L[:, oo] = np.where(k < rng.integers(1, 16, nc), y, W - 1)
        if z == 10:
            q = even(rng, 16, P); q[0] = q0; ch[q0 & 15, q0 >> 4] = R + i; p = rng.integers(1, 16, P); y = across(q)
            y = np.where(rng.random(P) < 0.25, y, (y & -16) + rng.integers(0, 15, P))
            L[:, R + i] = np.where(k == p, y, q)
        d[j] = [x, L, ch, q]
    return pack(d)
def setup_inputs_ties(rng):
    k = np.arange(16)[:, None]; i = np.arange(P); h = 3 * P // 4; s = np.where(i < h, i, i - P // 2); d = []
    for j in range(8 * N):
        x = look(rng); b = 16 * rng.integers(0, R - 1, 16) + np.arange(16)
        A = rng.permutation(W - 1); A = A[~np.isin(A, b)][:P]; B = b[np.where(rng.random(P) < 0.25, A & 15, rng.integers(0, 16, P))]; p = rng.integers(1, 16, P)
        x[:, b] = rng.integers(100, 121, (16, 16)); y = TH + rng.integers(-1, 2, P); v = rng.integers(-20, 21, (8, P))
        D = (y >> 4) + (k < (y & 15)) + np.concatenate([v, -v])
        f1 = rng.integers(0, 16, P); f2 = f1 ^ (1 << rng.integers(0, 4, P)); w = np.where(y > TH, 257, 259); z = y - w; o = k - (k > f1) - (k > f2)
        D = np.where(rng.random(P) < 0.5, D, np.where(k == f1, w >> 1, np.where(k == f2, w - (w >> 1), z // 14 + (o < z % 14))))
        x[:, A] = x[:, B] + D * np.where(D > 100, 1, rng.choice(np.array([-1, 1]), (16, P)))
        T = even(rng, 16, P); T[0] = apart(rng); T = T[:, s]
        L = np.full((16, M0), W - 1); ch = np.zeros((16, M0), np.int64)
        L[:, R:R + h] = np.where(k == p, A, T)[:, :h]; ch[T[0] & 15, T[0] >> 4] = R + s
        d.append([x, L, ch, np.where(k == p, B, T)])
    return pack(d)
def check_inputs(d):
    bad = []
    for a, lo, hi in (("desc", 0, 255), ("edge", 0, W - 1), ("child", 0, M0 - 1), ("req", 0, W - 2)):
        x = np.asarray(d[a]).astype(np.float64)
        if not (np.min(x) >= lo and np.max(x) <= hi): bad.append("range of " + a)
        if np.any(x != np.floor(x)): bad.append("whole numbers in " + a)
    c = np.sort(np.asarray(d["child"]).reshape(N, 8, 16 * M0), axis=-1)
    if np.any((c[..., 1:] == c[..., :-1]) & (c[..., 1:] > 0)): bad.append("a node stands twice in child")
    return bad
def walk(X, L, C, Q, rnd):
    i = np.arange(P); k = np.arange(16)[:, None]; n = M0 + 2 * P * rnd + 2 * i
    v = Q[0] >> 4; a = np.zeros(P, np.int64); on = np.ones(P, bool)
    for step in range(S):
        low = np.full(M, P); np.minimum.at(low, v[on], i[on])
        act = on & (low[v] == i)
        t = Q[np.minimum(a, 15), i] & 15; c = C[t, v]; E = L[:, c]; none = E == W - 1
        dist = np.add.reduce(np.abs(X[:, E] - X[:, Q]), axis=0)
        b = np.min(np.where((k >= a) & none, k, 16), axis=0)
        l = np.min(np.where((k >= a) & (none | (dist > TH)), k, 16), axis=0)
        leaf = act & ((c == 0) | ((l == a) & (l < b)))
        down = act & (c > 0) & (l == b)
        cut = act & (c > 0) & (l > a) & (l < b) & (low[c] == P)
        j = np.flatnonzero(cut); lj = l[j]; cj = c[j]; ej = E[lj, j]; qj = Q[lj, j]
        f = np.unique(qj, return_index=True)[1]
        X[:, qj[f]] = (X[:, qj[f]] + X[:, ej[f]]) >> 1
        L[:, n[j]] = np.where(k >= lj, E[:, j], W - 1); C[:, n[j]] = C[:, cj]
        L[:, cj] = np.where(k < lj, E[:, j], W - 1); C[:, cj] = 0; C[ej & 15, cj] = n[j]
        two = (ej & 15) != (qj & 15); o = j[two]
        C[qj[two] & 15, cj[two]] = n[o] + 1; L[:, n[o] + 1] = np.where(k >= l[o], Q[:, o], W - 1)
        j = np.flatnonzero(leaf)
        L[:, n[j]] = np.where(k >= a[j], Q[:, j], W - 1); C[t[j], v[j]] = n[j]
        v = np.where(down, c, v); a = np.where(down, b, a); on = on & ~leaf & ~cut & (a < 16)
    return a
def reference(desc, edge, child, req):
    X = desc.astype(np.float32).astype(np.int64).reshape(N, 8, 16, W); Q = req.astype(np.int64).reshape(N, 8, 16, P)
    L = np.full((N, 8, 16, M), W - 1); L[..., :M0] = edge.reshape(N, 8, 16, M0)
    C = np.zeros((N, 8, 16, M), np.int64); C[..., :M0] = child.reshape(N, 8, 16, M0)
    k = np.arange(1, 16)[:, None]; B = P // N
    for rnd in range(RO):
        new = np.zeros_like(Q)
        for r in range(N):
            for g in range(8):
                q = Q[r, g]; a = walk(X[r, g], L[r, g], C[r, g], q, rnd)
                h = ((q[1:] * q[:-1]) >> 5) & (W - 1); h = np.where(h == W - 1, 0, h)
                q = np.concatenate([q[:1], np.where(k >= a, h, q[1:])])
                for e in range(N): new[(r + e) % N, g, :, e * B:(e + 1) * B] = q[:, e * B:(e + 1) * B]
        Q = new
    return {"yd": X.reshape(N, 128, W).astype(np.float32).astype(BF), "ye": L.reshape(N, 128, M).astype(np.float32), "yr": Q.reshape(N, 128, P).astype(np.float32)}

@@ -1,0 +1,771 @@
+import math
+from concourse.mybir import dt, AluOpType, ActivationFunctionType
+from concourse.bass import DstId, RemoteDMATransfer
+
+F, H, BFL, I32, U16 = "float32", "float16", "bfloat16", "int32", "uint16"
+CFW = 16384 + 512 + 8192
+_S = {
+    "X": (4352, BFL), "LZ": (1792, F), "CF": (CFW, F), "BB": (2048, F), "OC0": (1792, BFL), "OC1": (1792, BFL),
+    "REQ": (256, I32), "CHI": (512, I32), "EDG": (512, I32), "CHH": (512, H),
+    "QX": (512, U16), "QN": (512, U16), "QI": (256, I32), "Q16": (256, U16),
+    "QZ": (256, F), "QK": (256, H), "QK0": (256, H), "QS": (256, H), "QR": (256, H), "QTI": (256, I32), "QTF": (256, F),
+    "HD": (256, F), "HI": (256, I32), "HM": (256, F),
+    "IPI": (16, I32), "KPI": (16, I32), "KC": (8, F), "ROWX": (128, F), "COLM": (128, F), "DIFF": (128, F), "COLX": (128, BFL),
+    "ONE": (256, BFL), "GB": (1024, BFL), "W0": (1024, BFL), "BIG": (1024, BFL), "GSEL": (8, BFL),
+    "BD2": (256, BFL), "SELA": (2048, BFL), "SELR": (2048, BFL), "IDB": (128, BFL), "NID": (128, BFL),
+    "LST": (128, BFL), "GEI": (128, BFL), "LW2": (128, BFL), "SP": (128, BFL), "SHF": (128, BFL),
+    "EXT": (152, F), "WO2": (16, F), "WB2": (128, F), "OHA0": (256, H), "ND": (512, F), "NDD": (512, F), "OV": (256, BFL), "MRW": (256, H),
+    "LDR": (16, F), "LDC": (16, F), "LDB": (16, F), "LDQ": (16, F), "LDL": (16, F), "ADR": (16, F), "KPN": (16, F),
+    "LI": (16, F), "DUM": (16, F), "DX": (16, F), "D12": (32, F), "NBD": (32, F), "DCN": (32, F), "CND": (32, F), "J16": (16, F),
+    "QD": (4096, BFL), "D4": (4096, BFL), "ED": (2048, BFL), "EQ": (3072, BFL), "AEQ": (1536, BFL),
+    "OHA": (256, H), "R1": (256, BFL), "R2": (256, BFL), "EZ": (256, F), "E16": (256, U16), "ES": (256, H), "G": (256, H),
+    "RM": (256, H), "QZA": (256, F), "QG": (256, H), "QKM": (256, H), "NN": (256, BFL), "KLB": (512, BFL), "MRB": (256, F),
+    "FG": (256, BFL), "OH": (256, H), "M3": (768, H), "OHC": (256, H), "T1": (256, F), "T2": (256, F), "T3": (256, F), "T4": (256, F),
+    "FR": (256, F), "AB": (512, BFL), "ABT": (512, BFL), "TM": (256, BFL), "RB": (384, BFL), "OG": (512, BFL), "BG": (256, H),
+    "FL": (256, H), "XQ": (256, BFL), "XA": (256, I32), "XB": (256, I32), "KP": (16, F), "YR": (256, F),
+    "ST": (48, F), "DF": (48, F), "Q3": (48, F), "VA16": (32, U16), "C16": (16, U16), "CO": (16, F), "NAH": (16, BFL),
+    "FTB": (64, BFL), "GEN": (128, BFL), "VMD": (16, F), "AL5": (16, F), "LF2": (16, F), "AL": (16, BFL), "AC": (16, F), "AT2": (16, F), "ACT": (16, F), "ATH": (16, F), "LF1": (16, F), "HC": (16, F), "NOC": (16, F),
+    "OLI": (16, F), "OL16": (16, U16), "CKH": (16, BFL), "NAQ": (16, F), "ZE": (16, F), "LAB": (32, F), "LCX": (16, F), "LD": (16, F),
+    "ADD": (16, F), "BX1": (16, F), "BX2": (16, F), "FUL": (16, F), "CC": (32, F), "FT": (32, F), "LF": (16, F), "DN": (16, F),
+    "SV": (16, BFL), "LQ": (32, I32), "LU": (32, U16), "RW": (32, I32), "RWF": (32, F), "A12": (32, F), "A12U": (32, U16), "LQT": (16, F),
+    "CL": (32, F), "CLU": (32, U16), "XF": (16, F), "XS": (16, F), "XSU": (16, U16), "KX": (16, F), "KXI": (16, I32), "KHI": (32, I32),
+    "KH": (32, H), "LFT": (32, H),
+}
+SCRATCH = {"P%d" % b: ("psum", [128, 512], "float32") for b in range(8)}
+_PLACE = {}
+_SMALL = {F: "SMF", H: "SMH", I32: "SMI", U16: "SMU", BFL: "SMB"}
+_fill = {}
+for _n in _S:
+    if _S[_n][0] <= 64:
+        _b = _SMALL[_S[_n][1]]
+        _PLACE[_n] = (_b, _fill.get(_b, 0))
+        _fill[_b] = _fill.get(_b, 0) + (_S[_n][0] + 15) // 16 * 16
+        SCRATCH[_b] = ("sbuf", [128, _fill[_b]], _S[_n][1])
+    else:
+        _PLACE[_n] = (_n, 0)
+        SCRATCH[_n] = ("sbuf", [128, _S[_n][0]], _S[_n][1])
+_LOADS = ["req", "child", "edge", "d0", "d1", "yd", "ye0", "ye1", "yr"]
+SEMAPHORES = ["sV", "sS", "sT", "sG", "arr0", "arr1", "loc"] + ["l_" + n for n in _LOADS]
+
+OP, FN = AluOpType, ActivationFunctionType
+
+
+def A(name, c0=0, c1=None, st=1):
+    b, o = _PLACE[name]
+    return (b, o + c0, o + (_S[name][0] if c1 is None else c1), st)
+
+
+WAKE, SLACK = 70.0, 0.0
+_ORDER = []
+EQS = 2
+ONV = 3
+
+
+def is_psum(name):
+    return name[0] == "P" and name[1:].isdigit()
+
+
+def PB(b, c0, c1, st=1):
+    return ("P%d" % b, c0, c1, st)
+
+
+def rank_program(g, core, T, topo):
+    rank = T.rank_of(core)
+    if rank is None:
+        return
+    N = len(T.cores)
+    queues = {"V": g.vector, "S": g.scalar, "T": g.tensor, "G": g, "Y": g.sync}
+    cnt, clock, hist = {}, {}, {}
+    known = {q: {} for q in queues}
+
+    def ap(x):
+        return T[x[0]][:, x[1]:x[2]:x[3]] if x[3] != 1 else T[x[0]][:, x[1]:x[2]]
+
+    def need(q, src, n):
+        if known[q].get(src, 0) >= n:
+            return
+        queues[q].wait_ge(T.sem[src], n)
+        for k, v in clock.get((src, n), {}).items():
+            if known[q].get(k, 0) < v:
+                known[q][k] = v
+        known[q][src] = n
+
+    nodes = []
+
+    def do(q, call, outs, ins, sem=None, inc=1, cost=100.0, lat=0.0):
+        nodes.append((q, call, outs, ins, sem, inc, cost, lat))
+
+    def order():
+        n = len(nodes)
+        succ, npre = [[] for _ in range(n)], [0] * n
+        last = {}
+        for i, (q, call, outs, ins, sem, inc, cost, lat) in enumerate(nodes):
+            pre = set()
+            for acc, w in [(x, False) for x in ins] + [(x, True) for x in outs]:
+                h = last.setdefault(acc[0], [])
+                ps = is_psum(acc[0])
+                for (lo, hi, hw, j) in h:
+                    if j != i and (ps or (lo < acc[2] and acc[1] < hi and (w or hw))):
+                        pre.add(j)
+                if ps:
+                    h[:] = [(0, 512, True, i)]
+                else:
+                    if w and acc[3] == 1:
+                        h[:] = [e for e in h if not (acc[1] <= e[0] and e[1] <= acc[2])]
+                    h.append((acc[1], acc[2], w, i))
+            for j in pre:
+                succ[j].append(i)
+            npre[i] = len(pre)
+        prio = [0.0] * n
+        for i in range(n - 1, -1, -1):
+            prio[i] = nodes[i][6] + nodes[i][7] + max([prio[j] + (0 if nodes[j][0] == "T" == nodes[i][0] else WAKE) for j in succ[i]], default=0.0)
+        pred = [[] for _ in range(n)]
+        for i in range(n):
+            for j in succ[i]:
+                pred[j].append(i)
+
+        def run(follow, left, prio, latency):
+            left, at, end = list(left), [0.0] * n, [0.0] * n
+            ready, free, res = {q: [] for q in queues}, {q: 0.0 for q in queues}, []
+            for i in range(n):
+                if left[i] == 0:
+                    ready[nodes[i][0]].append(i)
+            while len(res) < n:
+                best = None
+                for q in queues:
+                    if ready[q]:
+                        t = max(free[q], min(at[i] for i in ready[q]))
+                        if best is None or t < best[0]:
+                            best = (t, q)
+                t, q = best
+                i = max((i for i in ready[q] if at[i] <= t + SLACK), key=lambda i: (prio[i] - max(0.0, at[i] - t), -i))
+                t = max(t, at[i])
+                ready[q].remove(i)
+                res.append(i)
+                free[q] = end[i] = t + nodes[i][6]
+                for j in follow[i]:
+                    at[j] = max(at[j], end[i] + (nodes[i][7] if latency else 0.0) + (0 if nodes[j][0] == "T" == q else WAKE))
+                    left[j] -= 1
+                    if left[j] == 0:
+                        ready[nodes[j][0]].append(j)
+            return max(end), res, end
+
+        best = None
+        for _ in range(6):
+            span, res, end = run(succ, npre, prio, True)
+            if best is None or span < best[0]:
+                best = (span, res)
+            prio = run(pred, [len(x) for x in succ], end, False)[2]
+        return best[1]
+
+    def issue(q, call, outs, ins, sem=None, inc=1, cost=0.0, lat=0.0):
+        src = sem or "s" + q
+        deps = {}
+        for acc, w in [(x, False) for x in ins] + [(x, True) for x in outs]:
+            ps = is_psum(acc[0])
+            for (lo, hi, hw, hq, hs, hn) in hist.get(acc[0], []):
+                same = hq == q and sem is None and hs == "s" + q
+                if ps and not same:
+                    hit = True
+                else:
+                    hit = lo < acc[2] and acc[1] < hi and (w or hw)
+                    if same and q == "T":
+                        hit = False
+                if hit:
+                    deps[hs] = max(deps.get(hs, 0), hn)
+        for s in sorted(deps, key=lambda s: s == src):
+            need(q, s, deps[s])
+        ins_ = call(queues[q])
+        if sem in ("arr0", "arr1"):
+            cnt[sem] = inc
+            cnt["loc"] = cnt.get("loc", 0) + inc
+            hist.setdefault("QN", []).append((outs[0][1], outs[0][2], True, "R", sem, inc))
+            return
+        cnt[src] = cnt.get(src, 0) + inc
+        n = cnt[src]
+        ins_.then_inc(T.sem[src], inc)
+        snap = dict(known[q])
+        clock[(src, n)] = snap
+        for acc, w in [(x, False) for x in ins] + [(x, True) for x in outs]:
+            h = hist.setdefault(acc[0], [])
+            ps = is_psum(acc[0])
+            if ps:
+                h[:] = [e for e in h if e[3] == q and not (acc[1] <= e[0] and e[1] <= acc[2])]
+            elif w and acc[3] == 1:
+                h[:] = [e for e in h if not (acc[1] <= e[0] and e[1] <= acc[2])]
+            elif not w:
+                h[:] = [e for e in h if not (not e[2] and e[4] == src and acc[1] <= e[0] and e[1] <= acc[2])]
+            h.append((acc[1], acc[2], w, q, src, n))
+
+    def iap(x):
+        return ap(x[1]).indirect(ap(x[2])) if x[0] == "I" else ap(x)
+
+    def parts(*xs):
+        r = []
+        for x in xs:
+            if isinstance(x, tuple):
+                r += [x[1], x[2]] if x[0] == "I" else [x]
+        return r
+
+    def oparts(out, ins):
+        return ([out[1]], ins + [out[2]]) if out[0] == "I" else ([out], ins)
+
+    def wid(x):
+        return 16 * (x[2][2] - x[2][1]) if x[0] == "I" else (x[2] - x[1] + x[3] - 1) // x[3]
+
+    def vcost(out, *xs):
+        n = wid(out)
+        if out[0] == "I":
+            c = 3.8 * n
+        elif any(x[0] == "I" for x in xs):
+            c = 1.56 * n
+        elif len(xs) == 2:
+            c = n if any(is_psum(x[0]) for x in xs) else 2 * n
+        else:
+            c = n * (0.5 if all(SCRATCH[x[0]][2] in (H, BFL, U16) for x in (out, xs[0])) else 1)
+        return 62 + 1.04 * max(64, c)
+
+    def tt(out, a, b, op):
+        o, i = oparts(out, parts(a, b))
+        do("V", lambda e: e.tensor_tensor(iap(out), iap(a), iap(b), op), o, i, cost=vcost(out, a, b))
+
+    def ts(out, a, s1, op0, s2=None, op1=None):
+        o, i = oparts(out, parts(a, s1, s2))
+        v1 = ap(s1) if isinstance(s1, tuple) else s1
+        v2 = ap(s2) if isinstance(s2, tuple) else s2
+        if op1 is None:
+            do("V", lambda e: e.tensor_scalar(iap(out), iap(a), v1, None, op0), o, i, cost=vcost(out, a))
+        else:
+            do("V", lambda e: e.tensor_scalar(iap(out), iap(a), v1, v2, op0, op1), o, i, cost=vcost(out, a))
+
+    def cp(out, a):
+        o, i = oparts(out, parts(a))
+        do("V", lambda e: e.tensor_copy(iap(out), iap(a)), o, i, cost=vcost(out, a))
+
+    def fill(out, c):
+        do("V", lambda e: e.memset(ap(out), c), [out], [], cost=62 + 1.04 * wid(out))
+
+    def act(out, a, fn, scale=1.0, bias=0.0):
+        i = parts(a, scale, bias)
+        sc = ap(scale) if isinstance(scale, tuple) else scale
+        bi = ap(bias) if isinstance(bias, tuple) else bias
+        do("S", lambda e: e.activation(iap(out), iap(a), fn, bias=bi, scale=sc), [out], i,
+           cost=80 + 1.04 * wid(out) * (1.56 if a[0] == "I" else 1) + (1600 if fn == FN.Exp else 0))
+
+    def mm(out, lhsT, rhs, start=True, stop=True):
+        do("T", lambda e: e.matmul(ap(out), ap(lhsT), ap(rhs), start, stop), [out], [lhsT, rhs], cost=10 + 0.89 * max(64, wid(rhs)))
+
+    def iota(out, pattern, base, cm):
+        c = 160 + 2.08 * wid(out)
+        if SCRATCH[out[0]][2] == I32:
+            do("G", lambda e: e.iota(ap(out), pattern, base, cm), [out], [], cost=c)
+        else:
+            do("G", lambda e: e.iota(ap(out), pattern, base, cm, allow_small_or_imprecise_dtypes=True), [out], [], cost=c)
+
+    def load(q, name, buf, src):
+        do(q, lambda e: e.dma_start(ap(buf), src), [buf], [], sem="l_" + name, inc=16, lat=2000 + 2.0 * wid(buf))
+
+    def store(q, name, dst, buf):
+        do(q, lambda e: e.dma_start(dst, ap(buf)), [], [buf], sem="l_" + name, inc=16, lat=2000 + 2.0 * wid(buf))
+
+    VL16, AD16 = A("VA16", 0, 16), A("VA16", 16, 32)
+    rot = [0]
+
+    def nb():
+        rot[0] = (rot[0] + 1) % 5
+        return 3 + rot[0]
+
+    def SELA(p):
+        return A("SELA", 128 * p, 128 * p + 128)
+
+    def SELR(p):
+        return A("SELR", 128 * p, 128 * p + 128)
+
+    def conv(name, c0, w):
+        b = nb()
+        for p in range(16):
+            mm(PB(b, 0, w // 16), SELA(p), A(name, c0 + p, c0 + w, 16), p == 0, p == 15)
+        return b
+
+    def expand(b, name, w):
+        for q in range(16):
+            mm(PB(b, q, 16 * w, 16), SELR(q), A(name, 0, w))
+
+    def kc(j):
+        return A("KC", j, j + 1)
+
+    load("Y", "req", A("REQ"), T.req[:, :])
+    load("S", "child", A("CHI"), T.child[:, :])
+    load("Y", "d0", A("X", 0, 2048), T.desc[:, 0:2048])
+    load("S", "edge", A("EDG"), T.edge[:, :])
+    load("Y", "d1", A("X", 2048, 4096), T.desc[:, 2048:4096])
+    iota(A("IPI"), [[0, 16]], 0, 1)
+    iota(A("ROWX"), [[-16, 8], [0, 16]], 0, 1)
+    iota(A("COLM"), [[0, 8], [1, 16]], 1, 0)
+    iota(A("DIFF"), [[1, 128]], 0, -1)
+    iota(A("J16"), [[16, 16]], 0, 0)
+    iota(A("EXT", 0, 16), [[0, 2], [16, 8]], 0, 0)
+    iota(A("EXT", 16, 144), [[1, 128]], 0, 0)
+    iota(A("EXT", 144, 152), [[0, 8]], 0, 1)
+    iota(A("OC0"), [[0, 1792]], 0, 0)
+    iota(A("OC1"), [[0, 1792]], 0, 0)
+    iota(A("OV"), [[1, 256]], 1, 0)
+    GX, ZG = A("CF", 16896, 17920), A("CF", 17920, 18944)
+    iota(GX, [[-16, 8], [0, 128]], 0, 1)
+    iota(ZG, [[1, 8], [-1, 8], [0, 16]], 0, 0)
+    iota(A("ND", 0, 256), [[2, 256]], 512, 0)
+    iota(A("ND", 256, 512), [[2, 256]], 513, 0)
+    iota(A("CF", 8192, 16896), [[0, 8704]], 0, 0)
+    iota(A("BB"), [[1, 2048]], 0, 0)
+    iota(A("LZ", 512, 1792), [[0, 1280]], 0, 0)
+
+    ts(A("KPI"), A("IPI"), 15, OP.bitwise_and)
+    cp(kc(0), A("KPI", 0, 1))
+    ts(kc(1), A("KPI", 0, 1), -1.0, OP.mult, 16.0, OP.add)
+    ts(kc(2), A("KPI", 0, 1), -8192.0, OP.mult, 131072.0, OP.add)
+    ts(kc(3), A("KPI", 0, 1), 0.0, OP.is_gt)
+    ts(kc(6), A("KPI", 0, 1), 0.0, OP.is_equal)
+    ts(A("BD2", 0, 128), A("ROWX"), kc(0), OP.is_equal)
+    tt(A("COLX"), A("BD2", 0, 128), A("COLM"), OP.mult)
+    for p in range(16):
+        ts(SELA(p), A("COLX"), float(p + 1), OP.is_equal)
+
+    def requests(r):
+        src = "REQ" if r == 0 else "QN"
+        s0 = A(src, 0, 256)
+        ts(A("QTF"), s0, 2048.0, OP.is_ge, -2048.0, OP.add)
+        if r == 0:
+            cp(A("QI"), A("REQ"))
+        else:
+            cp(A("QI"), s0)
+        tt(A("QK"), A("QTF"), A("QI"), OP.add)
+        ts(A("QK0"), A("QK"), kc(6), OP.mult)
+        b = conv("QK0", 0, 256)
+        cp(A("Q16"), s0)
+        ts(A("LDR"), PB(b, 0, 16), 0.0, OP.is_gt, -2048.0, OP.add)
+        tt(A("LQ", 0, 16), PB(b, 0, 16), A("LDR"), OP.subtract)
+        ts(A("KXI"), A("LQ", 0, 16), 4, OP.arith_shift_right)
+        ts(A("LQ", 16, 32), A("LQ", 0, 16), 15, OP.bitwise_and)
+        cp(VL16, A("KXI"))
+        cp(A("ST", 0, 16), A("KXI"))
+
+    def requests2(r):
+        ts(A("QTI"), A("QI"), 15, OP.bitwise_and)
+        ts(A("QR"), A("QTI"), 512.0, OP.mult)
+        ts(A("QZ"), A("QI"), -1.0, OP.mult, 4095.0, OP.add)
+        ts(A("QG"), A("QK"), kc(3), OP.mult)
+
+    def hashes(r):
+        ts(A("QS"), A("QI"), -2048.0, OP.add)
+        b = nb()
+        mm(PB(b, 0, 256), A("SHF"), A("QS"))
+        cp(A("QTF"), A("QI"))
+        ts(A("HM"), PB(b, 0, 256), 2048.0, OP.add)
+        tt(A("HI"), A("HM"), A("QTF"), OP.mult)
+        ts(A("HI"), A("HI"), 5, OP.logical_shift_right, 4095, OP.bitwise_and)
+        ts(A("HM"), A("HI"), 4095.0, OP.is_lt)
+        tt(A("HM"), A("HM"), A("HI"), OP.mult)
+        tt(A("HD"), A("HM"), A("QTF"), OP.subtract)
+        ts(A("HD"), A("HD"), kc(3), OP.mult)
+
+    def queries(c):
+        act(A("QD", 1024 * c, 1024 * c + 1024), ("I", A("X", 0, 4096), A("Q16", 64 * c, 64 * c + 64)), FN.Copy)
+
+    def digits():
+        ts(A("KHI", 0, 16), A("KXI"), 4, OP.arith_shift_right)
+        ts(A("KHI", 16, 32), A("KXI"), 15, OP.bitwise_and)
+        cp(A("KH"), A("KHI"))
+
+    requests(0)
+    digits()
+    ts(A("RWF", 0, 16), A("LQ", 16, 32), 512.0, OP.mult)
+    for q in range(16):
+        ts(SELR(q), A("ROWX"), float(q), OP.is_equal)
+    cp(A("NAH"), A("LQ", 16, 32))
+    expand(2, "NAH", 16)
+    ts(A("RM"), PB(2, 0, 256), kc(0), OP.is_equal)
+    ts(A("IDB"), A("DIFF"), 0.0, OP.is_equal)
+    cp(A("CHH"), A("CHI"))
+    ts(A("LZ", 0, 512), A("EDG"), -1.0, OP.mult, 4095.0, OP.add)
+    for t in range(16):
+        b = nb()
+        mm(PB(b, 0, 512), SELR(t), A("CHH"))
+        if t % 4 == 3:
+            cp(A("CF", 512 * t, 512 * t + 512), PB(b, 0, 512))
+        else:
+            act(A("CF", 512 * t, 512 * t + 512), PB(b, 0, 512), FN.Copy)
+    cp(A("LDC"), A("KPI"))
+    tt(A("LI"), A("J16"), A("LDC"), OP.add)
+    tt(A("EXT", 0, 16), A("EXT", 0, 16), A("LDC"), OP.add)
+    ln = math.log(2.5)
+    ts(A("EXT", 0, 144), A("EXT", 0, 144), -ln, OP.mult, 64 * ln + math.log(2.0), OP.add)
+    ts(A("EXT", 144, 145), A("EXT", 144, 145), -ln, OP.mult, 64 * ln, OP.add)
+    ts(A("EXT", 145, 146), A("EXT", 145, 146), -ln / 2, OP.mult, 32 * ln, OP.add)
+    act(A("WO2"), A("EXT", 0, 16), FN.Exp)
+    act(A("WB2"), A("EXT", 16, 144), FN.Exp)
+    act(A("KC", 4, 6), A("EXT", 144, 146), FN.Exp)
+    cp(A("BD2", 128, 256), A("BD2", 0, 128))
+    ts(A("NID"), A("IDB"), -1.0, OP.mult)
+    ts(A("LST"), A("DIFF"), 0.0, OP.is_gt)
+    tt(A("LST"), A("LST"), A("BD2", 0, 128), OP.mult)
+    tt(A("GEI"), A("LST"), A("IDB"), OP.add)
+    ts(A("GEN"), A("GEI"), -1.0, OP.mult)
+    ts(A("LW2"), A("LST"), -2.0, OP.mult)
+    tt(A("SP"), A("IDB"), A("LW2"), OP.add)
+    ts(A("SHF"), A("DIFF"), 1.0, OP.is_equal)
+    ts(A("DUM"), A("LI"), 1536.0, OP.add)
+    ts(A("DX"), A("LI"), 4096.0, OP.add)
+    ts(A("D12", 0, 16), A("LI"), 16384.0, OP.add)
+    ts(A("D12", 16, 32), A("LI"), 16640.0, OP.add)
+    cp(A("DCN", 0, 16), A("DUM"))
+    ts(A("DCN", 16, 32), A("LI"), 1792.0, OP.add)
+    ts(A("GSEL"), GX[:3] + (128,), kc(0), OP.is_equal)
+    ts(A("GB"), GX, kc(0), OP.is_equal)
+    ts(A("W0"), ZG, 0.0, OP.is_equal, kc(4), OP.mult)
+    ts(A("BIG"), ZG, 0.0, OP.is_equal, 1e28, OP.mult)
+    fill(A("ONE"), 1.0)
+    fill(A("OHA0"), 1.0)
+    ts(A("OHA0"), A("OHA0"), kc(6), OP.mult)
+    requests2(0)
+    hashes(0)
+    for c in range(4):
+        queries(c)
+    for z in range(16896, CFW, 1024):
+        iota(A("CF", z, z + 1024), [[0, 1024]], 0, 0)
+
+    def step(r, s):
+        first, end, final = s == 0, s == 2, r == 1 and s == 2
+        stamp = 1 + 3 * r + s
+        nbase = 512 + 512 * r
+        boff = 7680.0 if r == 0 else 15872.0
+        nodes = 512 + 512 * r if first else 1024 + 512 * r
+        lzw = A("LZ", 0, nodes)
+        V_, AD_, NA_ = A("ST", 0, 16), A("ST", 16, 32), A("ST", 32, 48)
+        oha = "OHA0" if first else "OHA"
+        qza = "QZ" if first else "QZA"
+        if first:
+            fill(NA_, 16.0)
+            fill(A("AL"), 1.0)
+            tt(A("VMD"), V_, A("DUM"), OP.subtract)
+            ts(A("NBD", 0, 16), A("LI"), 2.0, OP.mult, nbase + boff, OP.add)
+            tt(A("NBD", 0, 16), A("NBD", 0, 16), A("D12", 0, 16), OP.subtract)
+            ts(A("NBD", 16, 32), A("NBD", 0, 16), -256.0, OP.add)
+            ts(A("CND", 16, 32), A("LI"), 2.0, OP.mult, float(nbase - 1792), OP.add)
+            tt(A("CND", 16, 32), A("CND", 16, 32), A("LI"), OP.subtract)
+            cp(A("NDD", 0, 256), A("ND", 0, 256))
+        if r == 0 and first:
+            tt(AD_, V_, A("RWF", 0, 16), OP.add)
+            tt(A("G"), ("I", A("CHI"), VL16), A("RM"), OP.mult)
+            b = conv("G", 0, 256)
+            ts(A("C16"), PB(b, 0, 16), 1.0, OP.mult)
+            act(A("CO"), PB(b, 0, 16), FN.Copy)
+        else:
+            cp(A("G"), ("I", A("CF", 0, 16896 if r == 0 else CFW), AD16))
+            b = conv("G", 0, 256)
+            ts(A("C16"), PB(b, 0, 16), 0.0625, OP.mult)
+            act(A("CO"), PB(b, 0, 16), FN.Copy, scale=0.0625)
+        expand(b4 := nb(), "KH", 32)
+        ts(A("AB"), PB(b4, 0, 512), kc(0), OP.is_equal)
+        ts(A("E16"), ("I", lzw, A("C16")), -1.0, OP.mult, 4095.0, OP.add)
+        b = nb()
+        for h in range(4):
+            mm(PB(b, 128 * h, 128 * h + 128), A("AB", 128 * h, 128 * h + 128), A("IDB"))
+        act(A("ABT"), PB(b, 0, 512), FN.Copy, scale=kc(5))
+        act(A("R2"), ("I", lzw, A("C16")), FN.Relu, scale=-8192.0, bias=8192.0)
+        if not first:
+            expand(2, "NAH", 16)
+            act(A("R1"), PB(2, 0, 256), FN.Relu, scale=-8192.0, bias=kc(2))
+            ts(A("OHA"), PB(2, 0, 256), kc(1), OP.is_equal)
+            b = nb()
+            mm(PB(b, 0, 256), A("GEI"), A("OHA"))
+            mm(PB(b, 256, 512), A("LST"), A("OHA"))
+            tt(A("QG"), PB(b, 256, 512), A("QK"), OP.mult)
+            tt(A("QZA"), PB(b, 0, 256), A("QZ"), OP.mult)
+        b = nb()
+        for h in range(2):
+            mm(PB(b, 128 * h, 128 * h + 128), A("ABT", 128 * h, 128 * h + 128), A("ABT", 256 + 128 * h, 384 + 128 * h))
+
+        def dist(c):
+            w = slice(64 * c, 64 * c + 64)
+            lo, hi = 1024 * c, 1024 * c + 1024
+            desc = ("I", A("X", 0, 4096), A("E16", w.start, w.stop))
+            if c < ONV:
+                tt(A("D4", lo, hi), desc, A("QD", lo, hi), OP.subtract)
+                act(A("D4", lo, hi), A("D4", lo, hi), FN.Abs)
+            else:
+                act(A("ED", lo % 2048, lo % 2048 + 1024), desc, FN.Copy)
+                for z in (0, 512):
+                    bz = nb()
+                    mm(PB(bz, 0, 512), A("IDB"), A("ED", lo % 2048 + z, lo % 2048 + z + 512), True, False)
+                    mm(PB(bz, 0, 512), A("NID"), A("QD", lo + z, lo + z + 512), False, True)
+                    act(A("D4", lo + z, lo + z + 512), PB(bz, 0, 512), FN.Abs)
+            o = PB(0, w.start, w.stop)
+            mm(o, A("NID"), A("R2", w.start, w.stop), True, False)
+            if not first:
+                mm(o, A("NID"), A("R1", w.start, w.stop), False, False)
+            for k in range(16):
+                mm(o, A("SELA", 128 * k, 128 * k + 128), A("D4", lo + k, hi, 16), False, k == 15)
+
+        tt(A("TM"), PB(b, 0, 256), A("BD2"), OP.mult)
+        b = nb()
+        mm(PB(b, 0, 128), A("TM", 0, 128), A("AB", 0, 128))
+        mm(PB(b, 128, 256), A("TM", 128, 256), A("AB", 128, 256))
+        mm(PB(b, 256, 384), A("TM", 0, 128), A("AB", 128, 256))
+        b2 = nb()
+        mm(PB(b2, 0, 256), A("IDB"), A("R2"), True, first)
+        if not first:
+            mm(PB(b2, 0, 256), A("NID"), A("R1"), False, True)
+        act(A("NN"), PB(b2, 0, 256), FN.Relu, scale=1.0 / 8192)
+        dist(0)
+        tt(A("RB", 0, 256), PB(b, 0, 256), A("AB", 256, 512), OP.mult)
+        tt(A("RB", 256, 384), PB(b, 256, 384), A("AB", 384, 512), OP.mult)
+        b = conv("RB", 0, 384)
+        tt(A("AC"), PB(b, 0, 16), A("WO2"), OP.is_lt)
+        ts(A("AT2", 0, 8), PB(b, 16, 24), 0.0, OP.is_equal)
+        tt(A("AC", 8, 16), A("AC", 8, 16), A("AT2", 0, 8), OP.mult)
+        tt(A("ACT"), A("AC"), A("AL"), OP.mult)
+        tt(A("OLI"), A("VMD"), A("ACT"), OP.mult)
+        tt(A("OLI"), A("OLI"), A("DUM"), OP.add)
+        cp(A("OL16"), A("OLI"))
+        b2 = nb()
+        mm(PB(b2, 0, 256), A("SP"), A("NN"))
+        act(A("KLB", 0, 256), PB(b2, 0, 256), FN.Relu, scale=kc(1))
+        if not end:
+            act(A("KLB", 256, 512), PB(b2, 0, 256), FN.Relu)
+        dist(1)
+        oc = "OC%d" % ((r + s) % 2)
+        cp(("I", A(oc), A("OL16")), A("OV"))
+        act(A("OG", 0, 256), ("I", A(oc), A("C16")), FN.Copy)
+        if not end:
+            act(A("OG", 256, 512), ("I", A(oc), VL16), FN.Copy)
+        if not final:
+            iota(A(oc), [[0, 1792]], 0, 0)
+        bo = conv("OG", 0, 256 if end else 512)
+        tt(A("ATH"), A("ACT"), A("CO"), OP.min)
+        tt(A("LF1"), A("ACT"), A("ATH"), OP.subtract)
+        tt(A("CKH"), PB(bo, 0, 16), A("ATH"), OP.is_lt)
+        act(A("NAQ"), A("ATH"), FN.Identity, scale=100.0, bias=-1.0)
+        tt(A("NAQ"), A("NAQ"), NA_, OP.min)
+        act(A("ZE"), A("ATH"), FN.Identity, bias=-1.0)
+        if not end:
+            act(A("LAB"), PB(bo, 0, 32), FN.Identity, scale=0.0625, bias=-1.0)
+            tt(A("LCX"), A("LAB", 0, 16), A("LAB", 16, 32), OP.subtract)
+        expand(bc := nb(), "CKH", 16)
+        tt(A("QKM"), PB(bc, 0, 256), A("QG"), OP.mult)
+        dist(2)
+        if not end:
+            bm = nb()
+            mm(PB(bm, 0, 256), A("IDB"), A("KLB", 256, 512))
+            tt(A("MRW"), PB(bm, 0, 256), A("QR"), OP.mult)
+        if not final:
+            act(A("NDD", 256, 512), ("I", A("BB", 0, nodes), A("C16")), FN.Copy)
+            if not end:
+                ts(A("BG"), A("NDD", 256, 512), 0.0625, OP.mult)
+        dist(3)
+        bb = conv("KLB", 0, 256)
+        tt(A("DF", 32, 48), PB(bb, 0, 16), NA_, OP.subtract)
+        ts(A("FUL"), PB(bb, 0, 16), 0.0, OP.is_equal)
+        if not end:
+            bg = nb()
+            for p in range(16):
+                mm(PB(bg, 16, 32), SELA(p), A("BG", p, 256, 16), p == 0, p == 15)
+            for p in range(16):
+                mm(PB(bg, 0, 16), SELA(p), A("BG", p, 256, 16), p == 0, False)
+            for p in range(16):
+                mm(PB(bg, 0, 16), SELA(p), A("MRW", p, 256, 16), False, p == 15)
+            ts(A("BX1"), PB(bg, 16, 32), 512.0, OP.is_ge, 7680.0, OP.mult)
+            if nodes > 1024:
+                ts(A("BX2"), PB(bg, 16, 32), 1024.0, OP.is_ge, 8192.0, OP.mult)
+                tt(A("BX1"), A("BX1"), A("BX2"), OP.add)
+            tt(A("BX1"), A("BX1"), AD_, OP.subtract)
+            tt(A("DF", 16, 32), PB(bg, 0, 16), A("BX1"), OP.add)
+            tt(A("DF", 0, 16), A("CO"), V_, OP.subtract)
+        tt(A("ADD"), AD_, A("D12", 0, 16), OP.subtract)
+        tt(A("CND", 0, 16), A("CO"), A("DUM"), OP.subtract)
+        ts(A("ES"), A("E16"), -2048.0, OP.add)
+        act(A("EZ"), ("I", lzw, A("C16")), FN.Copy)
+        mm(PB(1, 0, 256), A("LW2"), A("NN"), True, False)
+        ts(A("FG"), PB(0, 0, 256), 780.0, OP.is_gt)
+        mm(PB(1, 0, 256), A("SP"), A("FG"), False, True)
+        ts(A("OH"), PB(1, 0, 256), 0.0, OP.is_gt)
+        tt(A("M3", 0, 256), A("OH"), A("QKM"), OP.mult)
+        ts(A("M3", 512, 768), A("OH"), kc(1), OP.mult)
+        ts(A("OHC"), A("M3", 0, 256), 0.0, OP.not_equal)
+        tt(A("M3", 256, 512), A("OHC"), A("ES"), OP.mult)
+        bk = nb()
+        for h in range(2):
+            mm(PB(bk, 8 * h, 8 * h + 8), A("M3", 128 * h, 128 * h + 128), A("GSEL"))
+        cp(A("KP"), PB(bk, 0, 16))
+        act(A("KPN"), PB(bk, 0, 16), FN.Copy, scale=-1.0)
+        po = conv("M3", 0, 768)
+        MQ, ML, KL = PB(po, 0, 16), PB(po, 16, 32), PB(po, 32, 48)
+        ts(A("LDQ"), MQ, 0.0, OP.is_gt, -2048.0, OP.add)
+        ts(A("LQ", 0, 16), ML, 2048.0, OP.add)
+        tt(A("LQ", 16, 32), MQ, A("LDQ"), OP.subtract)
+        cp(A("LU"), A("LQ"))
+        CC, CC2, TWO, LF = A("FTB", 0, 16), A("FTB", 0, 32), A("FTB", 32, 48), A("FTB", 48, 64)
+        ts(CC, MQ, 0.0, OP.not_equal)
+        ts(A("FTB", 16, 32), MQ, 0.0, OP.not_equal)
+        tt(A("LF2"), KL, A("NAQ"), OP.is_equal)
+        tt(A("DN"), KL, A("ZE"), OP.is_equal)
+        act(A("XQ"), ("I", A("X", 0, 4096), A("LU", 16, 32)), FN.Copy)
+        bx = 2
+        mm(PB(bx, 0, 256), A("GEI"), A("OHC"))
+        mm(PB(bx, 256, 512), A("IDB"), A("ONE"), True, False)
+        mm(PB(bx, 256, 512), A("GEN"), A("OHC"), False, True)
+        for gp in (3, 2, 0, 1) if EQS == 2 else (3, 0, 1, 2):
+            bq = nb()
+            for z in range(2):
+                q = 2 * gp + z
+                mm(PB(bq, 256 * z, 256 * z + 256), A("GB", 128 * q, 128 * q + 128), A("M3", 0, 256))
+            for z in range(2):
+                q = 2 * gp + z
+                h0, h1 = PB(bq, 256 * z, 256 * z + 256), PB(bq, 256 * z + 128, 256 * z + 256)
+                if gp >= 4 - EQS:
+                    o = 384 * (q - 4)
+                    act(A("AEQ", o, o + 256), h0, FN.Abs, bias=A("KPN", q, q + 1))
+                    act(A("AEQ", o + 256, o + 384), h1, FN.Abs, bias=A("KPN", 8 + q, 9 + q))
+                else:
+                    ts(A("EQ", 384 * q, 384 * q + 256), h0, A("KP", q, q + 1), OP.is_equal)
+                    ts(A("EQ", 384 * q + 256, 384 * q + 384), h1, A("KP", 8 + q, 9 + q), OP.is_equal)
+        e0 = 768 * (2 - EQS)
+        act(A("EQ", 1536 + e0, 3072), A("AEQ", e0, 1536), FN.Relu, scale=-1.0, bias=1.0)
+        for q in range(8):
+            W, B_ = A("W0", 128 * q, 128 * q + 128), A("BIG", 128 * q, 128 * q + 128)
+            mm(PB(0, 0, 128), W, A("EQ", 384 * q, 384 * q + 128), q == 0, q == 7)
+            mm(PB(1, 0, 128), B_, A("EQ", 384 * q + 128, 384 * q + 256), q == 0, False)
+            mm(PB(1, 0, 128), W, A("EQ", 384 * q + 256, 384 * q + 384), False, q == 7)
+        tt(LF, A("LF2"), A("LF1"), OP.add)
+        ts(A("RW"), A("LQ"), 15, OP.bitwise_and)
+        tt(TWO, A("RW", 0, 16), A("RW", 16, 32), OP.not_equal)
+        tt(A("XA"), ("I", A("X", 0, 4096), A("LU", 0, 16)), A("XQ"), OP.add)
+        tt(A("FL", 0, 128), PB(0, 0, 128), A("WB2"), OP.is_lt)
+        tt(A("FL", 128, 256), PB(1, 0, 128), A("WB2"), OP.is_lt)
+        bf = conv("FL", 0, 256)
+        ts(A("XB"), A("XA"), 1, OP.arith_shift_right)
+        tt(A("XS"), A("LQ", 16, 32), A("DX"), OP.subtract)
+        tt(A("XF"), PB(bf, 0, 16), CC, OP.min)
+        tt(A("XS"), A("XS"), A("XF"), OP.mult)
+        tt(A("XS"), A("XS"), A("DX"), OP.add)
+        cp(A("XSU"), A("XS"))
+        cp(("I", A("X"), A("XSU")), A("XB"))
+        if not end:
+            for c in range(4):
+                queries(c)
+        tt(A("Q3", 32, 48), A("DF", 32, 48), A("DN"), OP.mult)
+        if not end:
+            tt(A("Q3", 16, 32), A("DF", 16, 32), A("DN"), OP.mult)
+            tt(A("Q3", 0, 16), A("DF", 0, 16), A("DN"), OP.mult)
+        adl = AD_
+        if not final:
+            ts(A("RWF"), A("RW"), 512.0, OP.mult)
+            tt(A("RWF"), A("RWF"), A("NBD"), OP.add)
+            tt(A("A12"), A("RWF"), A("FTB", 16, 48), OP.mult)
+            tt(A("A12"), A("A12"), A("D12"), OP.add)
+            tt(A("LDL"), LF, A("ADD"), OP.mult)
+            tt(A("A12", 0, 16), A("A12", 0, 16), A("LDL"), OP.add)
+            cp(A("A12U"), A("A12"))
+            cp(("I", A("CF", 0, 16896 if r == 0 else CFW), A("A12U")), A("ND"))
+        if end:
+            tt(NA_, NA_, A("Q3", 32, 48), OP.add)
+            act(A("NAH"), NA_, FN.Copy)
+        else:
+            tt(A("ST"), A("ST"), A("Q3"), OP.add)
+            cp(A("VA16"), A("ST", 0, 32))
+            act(A("NAH"), NA_, FN.Copy)
+            tt(A("VMD"), V_, A("DUM"), OP.subtract)
+            tt(A("SV"), A("DN"), A("FUL"), OP.mult)
+            ba = nb()
+            mm(PB(ba, 0, 16), A("IDB"), A("AL"), True, False)
+            mm(PB(ba, 0, 16), A("NID"), CC, False, False)
+            mm(PB(ba, 0, 16), A("NID"), LF, False, False)
+            mm(PB(ba, 0, 16), A("NID"), A("SV"), False, True)
+            act(A("AL"), PB(ba, 0, 16), FN.Copy)
+            act(A("AL5"), PB(ba, 0, 16), FN.Identity, scale=512.0, bias=-1.0)
+            tt(A("KX"), A("LCX"), A("DN"), OP.mult)
+            tt(A("KX"), A("KX"), A("LAB", 16, 32), OP.add)
+            tt(A("KXI"), A("KX"), A("AL5"), OP.min)
+            digits()
+        tt(A("CL"), A("CND"), CC2, OP.mult)
+        tt(A("CL"), A("CL"), A("DCN"), OP.add)
+        cp(A("CLU"), A("CL"))
+        tt(A("T1"), PB(bx, 0, 256), A("EZ"), OP.mult)
+        tt(A("T3"), PB(bx, 0, 256), A("QZ"), OP.mult)
+        tt(A("FR"), PB(bx, 256, 512), A("EZ"), OP.mult)
+        be = nb()
+        for q in range(16):
+            mm(PB(be, q, 512, 16), SELR(q), A("FTB", 32, 64))
+        even, odd = A("LZ", nbase, nbase + 512, 2), A("LZ", nbase + 1, nbase + 512, 2)
+        tt(PB(be, 256, 512), PB(be, 256, 512), A(qza), OP.mult)
+        if first:
+            tt(odd, PB(be, 0, 256), A("T3"), OP.mult)
+            tt(even, PB(be, 256, 512), A("T1"), OP.add)
+        else:
+            tt(PB(be, 0, 256), PB(be, 0, 256), A("T3"), OP.mult)
+            tt(odd, PB(be, 0, 256), odd, OP.add)
+            tt(PB(be, 256, 512), PB(be, 256, 512), A("T1"), OP.add)
+            tt(even, PB(be, 256, 512), even, OP.add)
+        cp(("I", A("LZ"), A("CLU", 0, 16)), A("FR"))
+        if not final:
+            cp(("I", A("BB"), A("CLU")), A("NDD"))
+
+    def travel(r):
+        expand(2, "NAH", 16)
+        ts(A("OHA"), PB(2, 0, 256), kc(1), OP.is_equal)
+        b = nb()
+        mm(PB(b, 0, 256), A("GEI"), A("OHA"))
+        tt(A("T1"), PB(b, 0, 256), A("HD"), OP.mult)
+        tt(A("T2"), A("T1"), A("QTF"), OP.add)
+        lo = 256 * r
+        qx = A("QX", lo, lo + 256)
+        cp(qx, A("T2"))
+        cp(A("QN", lo, lo + 32), A("QX", lo, lo + 32))
+        tr, free = [], {}
+        dsts = [(e, T.cores[(rank + e) % N]) for e in range(1, N)]
+        used = []
+        for e, d in sorted(dsts, key=lambda x: len(topo.engines(core, x[1]))):
+            es = [x for x in topo.engines(core, d) if x not in used][:2]
+            used += es
+            rid, pid, se = topo.addr(d)
+            c0 = lo + 32 * e
+            tr.append(RemoteDMATransfer(dst_ids=[DstId(rid=rid, pnc=pid)], dma_engine_mask=sum(1 << x for x in es),
+                                        remote_sem=T.sem["arr%d" % r], src=T.QX[:, c0:c0 + 32], dst=T.QN[:, c0:c0 + 32], alu_op=0))
+        do("G", lambda e: e.remote_dma_fused(tr, local_sem=T.sem["loc"]), [A("QN", lo + 32, lo + 256)], [qx],
+           sem="arr%d" % r, inc=len(used), cost=1500.0, lat=5000.0)
+
+    for s in range(3):
+        step(0, s)
+    travel(0)
+    iota(A("ND", 0, 256), [[2, 256]], 1024, 0)
+    iota(A("ND", 256, 512), [[2, 256]], 1025, 0)
+    requests(1)
+    digits()
+    cp(A("RWF", 0, 16), A("LQ", 16, 32))
+    cp(A("BG"), ("I", A("BB", 0, 1024), VL16))
+    b = conv("BG", 0, 256)
+    ts(A("BX1"), PB(b, 0, 16), 8192.0, OP.is_ge, 7680.0, OP.mult)
+    ts(A("LDB"), PB(b, 0, 16), 0.0625, OP.mult)
+    tt(A("LDB"), A("LDB"), A("BX1"), OP.add)
+    ts(A("RWF", 0, 16), A("RWF", 0, 16), 512.0, OP.mult)
+    tt(A("ST", 16, 32), A("LDB"), A("RWF", 0, 16), OP.add)
+    cp(AD16, A("ST", 16, 32))
+    for c in range(4):
+        queries(c)
+    requests2(1)
+    hashes(1)
+    for s in range(3):
+        step(1, s)
+    travel(1)
+    store("Y", "yd", T.yd[:, :], A("X", 0, 4096))
+    act(A("LZ", 0, 768), A("LZ", 0, 768), FN.Identity, scale=-1.0, bias=4095.0)
+    store("Y", "ye0", T.ye[:, 0:768], A("LZ", 0, 768))
+    ts(A("LZ", 768, 1536), A("LZ", 768, 1536), -1.0, OP.mult, 4095.0, OP.add)
+    store("Y", "ye1", T.ye[:, 768:1536], A("LZ", 768, 1536))
+    cp(A("YR"), A("QN", 256, 512))
+    store("Y", "yr", T.yr[:, :], A("YR"))
+    if not _ORDER:
+        _ORDER.append(order())
+    for i in _ORDER[0]:
+        issue(*nodes[i])
+    for sname in sorted(cnt):
+        need("G", sname, cnt[sname])

@@ -1,4 +1,5 @@
 import math
+import numpy as np
 from concourse.mybir import dt, AluOpType, ActivationFunctionType
 from concourse.bass import DstId, RemoteDMATransfer
 
@@ -10,21 +11,21 @@ _S = {
     "QX": (512, U16), "QN": (512, U16), "QI": (256, I32), "Q16": (256, U16),
     "QZ": (256, F), "QK": (256, H), "QK0": (256, H), "QS": (256, H), "QR": (256, H), "QTI": (256, I32), "QTF": (256, F),
     "HD": (256, F), "HI": (256, I32), "HM": (256, F),
-    "IPI": (16, I32), "KPI": (16, I32), "KC": (8, F), "ROWX": (128, F), "COLM": (128, F), "DIFF": (128, F), "COLX": (128, BFL),
-    "ONE": (256, BFL), "GB": (1024, BFL), "W0": (1024, BFL), "BIG": (1024, BFL), "GSEL": (8, BFL),
+    "IPI": (16, I32), "KPI": (16, I32), "KC": (8, F), "K0": (1, F), "ROWX": (128, F), "COLM": (128, F), "DIFF": (128, F), "COLX": (128, BFL),
+    "ONE": (256, BFL), "GB": (1024, BFL), "ZG": (240, F), "W0": (240, BFL), "BIG": (240, BFL), "GSEL": (8, BFL),
     "BD2": (256, BFL), "SELA": (2048, BFL), "SELR": (2048, BFL), "IDB": (128, BFL), "NID": (128, BFL),
     "LST": (128, BFL), "GEI": (128, BFL), "LW2": (128, BFL), "SP": (128, BFL), "SHF": (128, BFL),
-    "EXT": (152, F), "WO2": (16, F), "WB2": (128, F), "OHA0": (256, H), "ND": (512, F), "NDD": (512, F), "OV": (256, BFL), "MRW": (256, H),
+    "EXT": (152, F), "WO2": (16, F), "WB2": (128, F), "ND": (512, F), "NDD": (512, F), "OV": (256, BFL),
     "LDR": (16, F), "LDC": (16, F), "LDB": (16, F), "LDQ": (16, F), "LDL": (16, F), "ADR": (16, F), "KPN": (16, F),
     "LI": (16, F), "DUM": (16, F), "DX": (16, F), "D12": (32, F), "NBD": (32, F), "DCN": (32, F), "CND": (32, F), "J16": (16, F),
     "QD": (4096, BFL), "D4": (4096, BFL), "ED": (2048, BFL), "EQ": (3072, BFL), "AEQ": (1536, BFL),
-    "OHA": (256, H), "R1": (256, BFL), "R2": (256, BFL), "EZ": (256, F), "E16": (256, U16), "ES": (256, H), "G": (256, H),
-    "RM": (256, H), "QZA": (256, F), "QG": (256, H), "QKM": (256, H), "NN": (256, BFL), "KLB": (512, BFL), "MRB": (256, F),
+    "OHA": (256, BFL), "R1": (256, BFL), "R2": (256, BFL), "EZ": (256, F), "E16": (256, U16), "ES": (256, H), "G": (256, H),
+    "RM": (256, H), "QZA": (256, F), "QG": (256, H), "QKM": (256, H), "NN": (256, BFL), "KLB": (256, BFL), "CT": (768, H),
     "FG": (256, BFL), "OH": (256, H), "M3": (768, H), "OHC": (256, H), "T1": (256, F), "T2": (256, F), "T3": (256, F), "T4": (256, F),
     "FR": (256, F), "AB": (512, BFL), "ABT": (512, BFL), "TM": (256, BFL), "RB": (384, BFL), "OG": (512, BFL), "BG": (256, H),
-    "FL": (256, H), "XQ": (256, BFL), "XA": (256, I32), "XB": (256, I32), "KP": (16, F), "YR": (256, F),
+    "FL": (256, H), "XQ": (256, BFL), "XL": (256, BFL), "XB": (256, I32), "KP": (16, F), "YR": (256, F),
     "ST": (48, F), "DF": (48, F), "Q3": (48, F), "VA16": (32, U16), "C16": (16, U16), "CO": (16, F), "NAH": (16, BFL),
-    "FTB": (64, BFL), "GEN": (128, BFL), "VMD": (16, F), "AL5": (16, F), "LF2": (16, F), "AL": (16, BFL), "AC": (16, F), "AT2": (16, F), "ACT": (16, F), "ATH": (16, F), "LF1": (16, F), "HC": (16, F), "NOC": (16, F),
+    "FTB": (64, BFL), "GEN": (128, BFL), "TW0": (16, F), "SPH": (128, BFL), "OHT": (256, BFL), "VMD": (16, F), "ALV": (16, F), "AL5": (16, F), "LF2": (16, F), "AL": (16, BFL), "AC": (16, F), "AT2": (16, F), "ACT": (16, F), "ATH": (16, BFL), "LF1": (16, F), "HC": (16, F), "NOC": (16, F),
     "OLI": (16, F), "OL16": (16, U16), "CKH": (16, BFL), "NAQ": (16, F), "ZE": (16, F), "LAB": (32, F), "LCX": (16, F), "LD": (16, F),
     "ADD": (16, F), "BX1": (16, F), "BX2": (16, F), "FUL": (16, F), "CC": (32, F), "FT": (32, F), "LF": (16, F), "DN": (16, F),
     "SV": (16, BFL), "LQ": (32, I32), "LU": (32, U16), "RW": (32, I32), "RWF": (32, F), "A12": (32, F), "A12U": (32, U16), "LQT": (16, F),
@@ -55,18 +56,18 @@ def A(name, c0=0, c1=None, st=1):
     return (b, o + c0, o + (_S[name][0] if c1 is None else c1), st)
 
 
-WAKE, SLACK = 70.0, 0.0
+WAKE, SLACK = 70.0, 60.0
+SETS = [(5, 0.9, 1.56, 3.8, 0.75, 70, 182.0), (0, 0.85, 1.2, 2.2, 0.6, 40, 150.0), (0, 0.9, 2.0, 5.5, 0.65, 60, 200.0),
+        (0, 0.9, 1.5, 3.5, 0.45, 40, 165.0), (10, 0.85, 1.5, 3.8, 0.6, 130, 190.0)]
+PASSES, SEEDS, KEPT = 6, (), []
 _ORDER = []
+CFV = 17
 EQS = 2
-ONV = 3
+ONV = 4
 
 
 def is_psum(name):
     return name[0] == "P" and name[1:].isdigit()
-
-
-def PB(b, c0, c1, st=1):
-    return ("P%d" % b, c0, c1, st)
 
 
 def rank_program(g, core, T, topo):
@@ -78,7 +79,11 @@ def rank_program(g, core, T, topo):
     cnt, clock, hist = {}, {}, {}
     known = {q: {} for q in queues}
 
+    def real(x):
+        return (_ORDER[0][1][x[0]],) + x[1:] if is_psum(x[0]) else x
+
     def ap(x):
+        x = real(x)
         return T[x[0]][:, x[1]:x[2]:x[3]] if x[3] != 1 else T[x[0]][:, x[1]:x[2]]
 
     def need(q, src, n):
@@ -92,14 +97,18 @@ def rank_program(g, core, T, topo):
 
     nodes = []
 
-    def do(q, call, outs, ins, sem=None, inc=1, cost=100.0, lat=0.0):
-        nodes.append((q, call, outs, ins, sem, inc, cost, lat))
+    def price(k, z):
+        a = SETS[z]
+        return k[0] + k[1] * a[0] + a[1] * (k[2] + k[3] * a[2] + k[4] * a[3]) + k[5] * a[4]
+
+    def do(q, call, outs, ins, sem=None, inc=1, cost=(100.0, 0, 0, 0, 0, 0), lat=0.0):
+        nodes.append((q, call, outs, ins, sem, inc, price(cost, 0), lat, cost))
 
     def order():
         n = len(nodes)
         succ, npre = [[] for _ in range(n)], [0] * n
         last = {}
-        for i, (q, call, outs, ins, sem, inc, cost, lat) in enumerate(nodes):
+        for i, (q, call, outs, ins, sem, inc, cost, lat, parts_) in enumerate(nodes):
             pre = set()
             for acc, w in [(x, False) for x in ins] + [(x, True) for x in outs]:
                 h = last.setdefault(acc[0], [])
@@ -124,42 +133,106 @@ def rank_program(g, core, T, topo):
             for j in succ[i]:
                 pred[j].append(i)
 
-        def run(follow, left, prio, latency):
+        banks = [sorted(set(x[0] for x in nd[2] + nd[3] if is_psum(x[0]))) for nd in nodes]
+        uses = {}
+        for bs in banks:
+            for b in bs:
+                uses[b] = uses.get(b, 0) + 1
+
+        def run(follow, left, prio, latency, limited):
             left, at, end = list(left), [0.0] * n, [0.0] * n
             ready, free, res = {q: [] for q in queues}, {q: 0.0 for q in queues}, []
+            idle, has, rest = {"P%d" % b: 0.0 for b in range(8)}, {}, dict(uses)
             for i in range(n):
                 if left[i] == 0:
                     ready[nodes[i][0]].append(i)
+
+            def when(i):
+                if limited:
+                    new = [b for b in banks[i] if b not in has]
+                    if new:
+                        if len(idle) < len(new):
+                            return 1e12
+                        return max(at[i], sorted(idle.values())[len(new) - 1] + WAKE)
+                return at[i]
+
             while len(res) < n:
                 best = None
                 for q in queues:
                     if ready[q]:
-                        t = max(free[q], min(at[i] for i in ready[q]))
+                        t = max(free[q], min(when(i) for i in ready[q]))
                         if best is None or t < best[0]:
                             best = (t, q)
                 t, q = best
-                i = max((i for i in ready[q] if at[i] <= t + SLACK), key=lambda i: (prio[i] - max(0.0, at[i] - t), -i))
-                t = max(t, at[i])
+                if t >= 1e12:
+                    return 1e12, res, end, has
+                i = max((i for i in ready[q] if when(i) <= t + SLACK), key=lambda i: (prio[i] - max(0.0, when(i) - t), -i))
+                t = max(t, when(i))
                 ready[q].remove(i)
                 res.append(i)
                 free[q] = end[i] = t + nodes[i][6]
+                if limited:
+                    for b in banks[i]:
+                        if b not in has:
+                            has[b] = min(idle, key=lambda z: (idle[z], z))
+                            del idle[has[b]]
+                        rest[b] -= 1
+                        if rest[b] == 0:
+                            idle[has[b]] = end[i]
                 for j in follow[i]:
                     at[j] = max(at[j], end[i] + (nodes[i][7] if latency else 0.0) + (0 if nodes[j][0] == "T" == q else WAKE))
                     left[j] -= 1
                     if left[j] == 0:
                         ready[nodes[j][0]].append(j)
-            return max(end), res, end
+            return max(end), res, end, has
+
+        def length(res, has, z):
+            wake = SETS[z][5]
+            end, qend, bend, opened = [0.0] * n, {q: 0.0 for q in queues}, {}, {}
+            for i in res:
+                nd = nodes[i]
+                q, t = nd[0], qend[nd[0]]
+                for j in pred[i]:
+                    u = end[j] + nodes[j][7] + (0 if q == "T" == nodes[j][0] else wake)
+                    if u > t:
+                        t = u
+                for b in banks[i]:
+                    if b not in opened:
+                        opened[b] = True
+                        t = max(t, bend.get(has[b], 0.0) + wake)
+                c = COSTS[z][i]
+                end[i] = qend[q] = t + c
+                for b in banks[i]:
+                    bend[has[b]] = max(bend.get(has[b], 0.0), t + c)
+            return max(end)
+
+        COSTS = [[nd[6] if z == 0 else price(nd[8], z) for nd in nodes] for z in range(len(SETS))]
+
+        def score(res, has):
+            return sum(length(res, has, z) / SETS[z][6] for z in range(len(SETS)))
 
         best = None
-        for _ in range(6):
-            span, res, end = run(succ, npre, prio, True)
-            if best is None or span < best[0]:
-                best = (span, res)
-            prio = run(pred, [len(x) for x in succ], end, False)[2]
-        return best[1]
+        for k in range(PASSES + len(SEEDS)):
+            if k >= PASSES:
+                rng = np.random.default_rng(SEEDS[k - PASSES])
+                z = rng.normal(0.0, 1.0, n) * (rng.random(n) < rng.choice([0.02, 0.1, 0.5])) * rng.choice([300.0, 1500.0])
+                prio = [a + float(b) for a, b in zip(best[3], z)]
+            span, res, end, has = run(succ, npre, prio, True, True)
+            if span < 1e12:
+                sc = score(res, has)
+                if best is None or sc < best[0]:
+                    best = (sc, res, has, prio)
+                    if k >= PASSES:
+                        KEPT.append((sc, SEEDS[k - PASSES]))
+            if k < PASSES:
+                if span >= 1e12:
+                    end = run(succ, npre, prio, True, False)[2]
+                prio = run(pred, [len(x) for x in succ], end, False, False)[2]
+        return best[1], best[2]
 
-    def issue(q, call, outs, ins, sem=None, inc=1, cost=0.0, lat=0.0):
+    def issue(q, call, outs, ins, sem=None, inc=1):
         src = sem or "s" + q
+        outs, ins = [real(x) for x in outs], [real(x) for x in ins]
         deps = {}
         for acc, w in [(x, False) for x in ins] + [(x, True) for x in outs]:
             ps = is_psum(acc[0])
@@ -216,14 +289,14 @@ def rank_program(g, core, T, topo):
     def vcost(out, *xs):
         n = wid(out)
         if out[0] == "I":
-            c = 3.8 * n
+            return (50, 0, 0, 0, n, 0)
         elif any(x[0] == "I" for x in xs):
-            c = 1.56 * n
+            return (50, 0, 0, n, 0, 0)
         elif len(xs) == 2:
             c = n if any(is_psum(x[0]) for x in xs) else 2 * n
         else:
-            c = n * (0.5 if all(SCRATCH[x[0]][2] in (H, BFL, U16) for x in (out, xs[0])) else 1)
-        return 62 + 1.04 * max(64, c)
+            c = n * (0.5 if all(not is_psum(x[0]) and SCRATCH[x[0]][2] in (H, BFL, U16) for x in (out, xs[0])) else 1)
+        return (0, 1, max(64, c), 0, 0, 0)
 
     def tt(out, a, b, op):
         o, i = oparts(out, parts(a, b))
@@ -243,20 +316,20 @@ def rank_program(g, core, T, topo):
         do("V", lambda e: e.tensor_copy(iap(out), iap(a)), o, i, cost=vcost(out, a))
 
     def fill(out, c):
-        do("V", lambda e: e.memset(ap(out), c), [out], [], cost=62 + 1.04 * wid(out))
+        do("V", lambda e: e.memset(ap(out), c), [out], [], cost=(0, 1, max(64, wid(out)), 0, 0, 0))
 
     def act(out, a, fn, scale=1.0, bias=0.0):
         i = parts(a, scale, bias)
         sc = ap(scale) if isinstance(scale, tuple) else scale
         bi = ap(bias) if isinstance(bias, tuple) else bias
         do("S", lambda e: e.activation(iap(out), iap(a), fn, bias=bi, scale=sc), [out], i,
-           cost=80 + 1.04 * wid(out) * (1.56 if a[0] == "I" else 1) + (1600 if fn == FN.Exp else 0))
+           cost=(65, 0, 0, wid(out), 0, 0) if a[0] == "I" else (1600 if fn == FN.Exp else 0, 1, max(64, wid(out)), 0, 0, 0))
 
     def mm(out, lhsT, rhs, start=True, stop=True):
-        do("T", lambda e: e.matmul(ap(out), ap(lhsT), ap(rhs), start, stop), [out], [lhsT, rhs], cost=10 + 0.89 * max(64, wid(rhs)))
+        do("T", lambda e: e.matmul(ap(out), ap(lhsT), ap(rhs), start, stop), [out], [lhsT, rhs], cost=(0, 0, 0, 0, 0, max(64, wid(rhs))))
 
     def iota(out, pattern, base, cm):
-        c = 160 + 2.08 * wid(out)
+        c = (160 + 2.08 * wid(out), 0, 0, 0, 0, 0)
         if SCRATCH[out[0]][2] == I32:
             do("G", lambda e: e.iota(ap(out), pattern, base, cm), [out], [], cost=c)
         else:
@@ -269,11 +342,20 @@ def rank_program(g, core, T, topo):
         do(q, lambda e: e.dma_start(dst, ap(buf)), [], [buf], sem="l_" + name, inc=16, lat=2000 + 2.0 * wid(buf))
 
     VL16, AD16 = A("VA16", 0, 16), A("VA16", 16, 32)
-    rot = [0]
+    rot = [7]
 
     def nb():
-        rot[0] = (rot[0] + 1) % 5
-        return 3 + rot[0]
+        rot[0] += 1
+        return rot[0]
+
+    cur = {}
+
+    def renew(*bs):
+        for b in bs:
+            cur[b] = nb()
+
+    def PB(b, c0, c1, st=1):
+        return ("P%d" % cur.get(b, b), c0, c1, st)
 
     def SELA(p):
         return A("SELA", 128 * p, 128 * p + 128)
@@ -310,9 +392,8 @@ def rank_program(g, core, T, topo):
     iota(A("OC0"), [[0, 1792]], 0, 0)
     iota(A("OC1"), [[0, 1792]], 0, 0)
     iota(A("OV"), [[1, 256]], 1, 0)
-    GX, ZG = A("CF", 16896, 17920), A("CF", 17920, 18944)
-    iota(GX, [[-16, 8], [0, 128]], 0, 1)
-    iota(ZG, [[1, 8], [-1, 8], [0, 16]], 0, 0)
+    iota(A("GB"), [[-16, 8], [0, 128]], 0, 1)
+    iota(A("ZG"), [[1, 15], [0, 16]], -7, 0)
     iota(A("ND", 0, 256), [[2, 256]], 512, 0)
     iota(A("ND", 256, 512), [[2, 256]], 513, 0)
     iota(A("CF", 8192, 16896), [[0, 8704]], 0, 0)
@@ -324,7 +405,7 @@ def rank_program(g, core, T, topo):
     ts(kc(1), A("KPI", 0, 1), -1.0, OP.mult, 16.0, OP.add)
     ts(kc(2), A("KPI", 0, 1), -8192.0, OP.mult, 131072.0, OP.add)
     ts(kc(3), A("KPI", 0, 1), 0.0, OP.is_gt)
-    ts(kc(6), A("KPI", 0, 1), 0.0, OP.is_equal)
+    ts(A("K0"), A("KPI", 0, 1), 0.0, OP.is_equal)
     ts(A("BD2", 0, 128), A("ROWX"), kc(0), OP.is_equal)
     tt(A("COLX"), A("BD2", 0, 128), A("COLM"), OP.mult)
     for p in range(16):
@@ -339,7 +420,7 @@ def rank_program(g, core, T, topo):
         else:
             cp(A("QI"), s0)
         tt(A("QK"), A("QTF"), A("QI"), OP.add)
-        ts(A("QK0"), A("QK"), kc(6), OP.mult)
+        ts(A("QK0"), A("QK"), A("K0"), OP.mult)
         b = conv("QK0", 0, 256)
         cp(A("Q16"), s0)
         ts(A("LDR"), PB(b, 0, 16), 0.0, OP.is_gt, -2048.0, OP.add)
@@ -359,14 +440,14 @@ def rank_program(g, core, T, topo):
         ts(A("QS"), A("QI"), -2048.0, OP.add)
         b = nb()
         mm(PB(b, 0, 256), A("SHF"), A("QS"))
-        cp(A("QTF"), A("QI"))
-        ts(A("HM"), PB(b, 0, 256), 2048.0, OP.add)
-        tt(A("HI"), A("HM"), A("QTF"), OP.mult)
+        act(PB(b, 256, 512), PB(b, 0, 256), FN.Identity, bias=2048.0)
+        tt(A("HI"), PB(b, 256, 512), A("QI"), OP.mult)
         ts(A("HI"), A("HI"), 5, OP.logical_shift_right, 4095, OP.bitwise_and)
-        ts(A("HM"), A("HI"), 4095.0, OP.is_lt)
-        tt(A("HM"), A("HM"), A("HI"), OP.mult)
-        tt(A("HD"), A("HM"), A("QTF"), OP.subtract)
-        ts(A("HD"), A("HD"), kc(3), OP.mult)
+        b = nb()
+        ts(PB(b, 0, 256), A("HI"), 4095.0, OP.is_lt, kc(3), OP.mult)
+        tt(PB(b, 0, 256), PB(b, 0, 256), A("HI"), OP.mult)
+        ts(A("HM"), A("QI"), kc(3), OP.mult)
+        tt(A("HD"), PB(b, 0, 256), A("HM"), OP.subtract)
 
     def queries(c):
         act(A("QD", 1024 * c, 1024 * c + 1024), ("I", A("X", 0, 4096), A("Q16", 64 * c, 64 * c + 64)), FN.Copy)
@@ -382,6 +463,7 @@ def rank_program(g, core, T, topo):
     for q in range(16):
         ts(SELR(q), A("ROWX"), float(q), OP.is_equal)
     cp(A("NAH"), A("LQ", 16, 32))
+    renew(2)
     expand(2, "NAH", 16)
     ts(A("RM"), PB(2, 0, 256), kc(0), OP.is_equal)
     ts(A("IDB"), A("DIFF"), 0.0, OP.is_equal)
@@ -390,7 +472,7 @@ def rank_program(g, core, T, topo):
     for t in range(16):
         b = nb()
         mm(PB(b, 0, 512), SELR(t), A("CHH"))
-        if t % 4 == 3:
+        if t % CFV == CFV - 1:
             cp(A("CF", 512 * t, 512 * t + 512), PB(b, 0, 512))
         else:
             act(A("CF", 512 * t, 512 * t + 512), PB(b, 0, 512), FN.Copy)
@@ -412,6 +494,9 @@ def rank_program(g, core, T, topo):
     ts(A("GEN"), A("GEI"), -1.0, OP.mult)
     ts(A("LW2"), A("LST"), -2.0, OP.mult)
     tt(A("SP"), A("IDB"), A("LW2"), OP.add)
+    ts(A("SPH"), A("SP"), 0.5, OP.mult)
+    fill(kc(7), -780.5)
+    ts(kc(6), kc(1), -1.0, OP.mult)
     ts(A("SHF"), A("DIFF"), 1.0, OP.is_equal)
     ts(A("DUM"), A("LI"), 1536.0, OP.add)
     ts(A("DX"), A("LI"), 4096.0, OP.add)
@@ -419,13 +504,11 @@ def rank_program(g, core, T, topo):
     ts(A("D12", 16, 32), A("LI"), 16640.0, OP.add)
     cp(A("DCN", 0, 16), A("DUM"))
     ts(A("DCN", 16, 32), A("LI"), 1792.0, OP.add)
-    ts(A("GSEL"), GX[:3] + (128,), kc(0), OP.is_equal)
-    ts(A("GB"), GX, kc(0), OP.is_equal)
-    ts(A("W0"), ZG, 0.0, OP.is_equal, kc(4), OP.mult)
-    ts(A("BIG"), ZG, 0.0, OP.is_equal, 1e28, OP.mult)
+    ts(A("GB"), A("GB"), kc(0), OP.is_equal)
+    cp(A("GSEL"), A("GB", 0, 1024, 128))
+    ts(A("W0"), A("ZG"), 0.0, OP.is_equal, kc(4), OP.mult)
+    ts(A("BIG"), A("ZG"), 0.0, OP.is_equal, 1e28, OP.mult)
     fill(A("ONE"), 1.0)
-    fill(A("OHA0"), 1.0)
-    ts(A("OHA0"), A("OHA0"), kc(6), OP.mult)
     requests2(0)
     hashes(0)
     for c in range(4):
@@ -446,7 +529,7 @@ def rank_program(g, core, T, topo):
         if first:
             fill(NA_, 16.0)
             fill(A("AL"), 1.0)
-            tt(A("VMD"), V_, A("DUM"), OP.subtract)
+            tt(A("ALV"), V_, A("DUM"), OP.subtract)
             ts(A("NBD", 0, 16), A("LI"), 2.0, OP.mult, nbase + boff, OP.add)
             tt(A("NBD", 0, 16), A("NBD", 0, 16), A("D12", 0, 16), OP.subtract)
             ts(A("NBD", 16, 32), A("NBD", 0, 16), -256.0, OP.add)
@@ -471,11 +554,14 @@ def rank_program(g, core, T, topo):
         for h in range(4):
             mm(PB(b, 128 * h, 128 * h + 128), A("AB", 128 * h, 128 * h + 128), A("IDB"))
         act(A("ABT"), PB(b, 0, 512), FN.Copy, scale=kc(5))
-        act(A("R2"), ("I", lzw, A("C16")), FN.Relu, scale=-8192.0, bias=8192.0)
+        act(A("EZ"), ("I", lzw, A("C16")), FN.Copy)
+        act(A("R2"), A("EZ"), FN.Relu, scale=-8192.0, bias=8192.0)
         if not first:
+            renew(2)
             expand(2, "NAH", 16)
             act(A("R1"), PB(2, 0, 256), FN.Relu, scale=-8192.0, bias=kc(2))
-            ts(A("OHA"), PB(2, 0, 256), kc(1), OP.is_equal)
+            act(A("OHT"), PB(2, 0, 256), FN.Abs, bias=kc(6))
+            act(A("OHA"), A("OHT"), FN.Relu, scale=-1.0, bias=1.0)
             b = nb()
             mm(PB(b, 0, 256), A("GEI"), A("OHA"))
             mm(PB(b, 256, 512), A("LST"), A("OHA"))
@@ -506,6 +592,7 @@ def rank_program(g, core, T, topo):
             for k in range(16):
                 mm(o, A("SELA", 128 * k, 128 * k + 128), A("D4", lo + k, hi, 16), False, k == 15)
 
+        renew(0)
         tt(A("TM"), PB(b, 0, 256), A("BD2"), OP.mult)
         b = nb()
         mm(PB(b, 0, 128), A("TM", 0, 128), A("AB", 0, 128))
@@ -524,14 +611,16 @@ def rank_program(g, core, T, topo):
         ts(A("AT2", 0, 8), PB(b, 16, 24), 0.0, OP.is_equal)
         tt(A("AC", 8, 16), A("AC", 8, 16), A("AT2", 0, 8), OP.mult)
         tt(A("ACT"), A("AC"), A("AL"), OP.mult)
-        tt(A("OLI"), A("VMD"), A("ACT"), OP.mult)
+        tt(A("ATH"), A("ACT"), A("CO"), OP.min)
+        expand(bc := nb(), "ATH", 16)
+        tt(A("OLI"), A("ALV"), A("AC"), OP.mult)
         tt(A("OLI"), A("OLI"), A("DUM"), OP.add)
         cp(A("OL16"), A("OLI"))
         b2 = nb()
         mm(PB(b2, 0, 256), A("SP"), A("NN"))
-        act(A("KLB", 0, 256), PB(b2, 0, 256), FN.Relu, scale=kc(1))
+        ts(A("CT", 0, 256), PB(b2, 0, 256), kc(1), OP.mult, 0.0, OP.max)
         if not end:
-            act(A("KLB", 256, 512), PB(b2, 0, 256), FN.Relu)
+            act(A("KLB"), PB(b2, 0, 256), FN.Relu)
         dist(1)
         oc = "OC%d" % ((r + s) % 2)
         cp(("I", A(oc), A("OL16")), A("OV"))
@@ -540,62 +629,58 @@ def rank_program(g, core, T, topo):
             act(A("OG", 256, 512), ("I", A(oc), VL16), FN.Copy)
         if not final:
             iota(A(oc), [[0, 1792]], 0, 0)
-        bo = conv("OG", 0, 256 if end else 512)
-        tt(A("ATH"), A("ACT"), A("CO"), OP.min)
+        if not end:
+            bo = conv("OG", 0, 512)
+        tt(PB(bc, 0, 256), PB(bc, 0, 256), A("OG", 0, 256), OP.is_gt)
         tt(A("LF1"), A("ACT"), A("ATH"), OP.subtract)
-        tt(A("CKH"), PB(bo, 0, 16), A("ATH"), OP.is_lt)
         act(A("NAQ"), A("ATH"), FN.Identity, scale=100.0, bias=-1.0)
         tt(A("NAQ"), A("NAQ"), NA_, OP.min)
         act(A("ZE"), A("ATH"), FN.Identity, bias=-1.0)
         if not end:
             act(A("LAB"), PB(bo, 0, 32), FN.Identity, scale=0.0625, bias=-1.0)
             tt(A("LCX"), A("LAB", 0, 16), A("LAB", 16, 32), OP.subtract)
-        expand(bc := nb(), "CKH", 16)
         tt(A("QKM"), PB(bc, 0, 256), A("QG"), OP.mult)
         dist(2)
         if not end:
             bm = nb()
-            mm(PB(bm, 0, 256), A("IDB"), A("KLB", 256, 512))
-            tt(A("MRW"), PB(bm, 0, 256), A("QR"), OP.mult)
+            mm(PB(bm, 0, 256), A("IDB"), A("KLB"))
+            tt(A("CT", 512, 768), PB(bm, 0, 256), A("QR"), OP.mult)
         if not final:
             act(A("NDD", 256, 512), ("I", A("BB", 0, nodes), A("C16")), FN.Copy)
             if not end:
-                ts(A("BG"), A("NDD", 256, 512), 0.0625, OP.mult)
+                ts(A("CT", 256, 512), A("NDD", 256, 512), 0.0625, OP.mult)
         dist(3)
-        bb = conv("KLB", 0, 256)
+        bb = conv("CT", 0, 256 if end else 768)
         tt(A("DF", 32, 48), PB(bb, 0, 16), NA_, OP.subtract)
         ts(A("FUL"), PB(bb, 0, 16), 0.0, OP.is_equal)
         if not end:
-            bg = nb()
-            for p in range(16):
-                mm(PB(bg, 16, 32), SELA(p), A("BG", p, 256, 16), p == 0, p == 15)
-            for p in range(16):
-                mm(PB(bg, 0, 16), SELA(p), A("BG", p, 256, 16), p == 0, False)
-            for p in range(16):
-                mm(PB(bg, 0, 16), SELA(p), A("MRW", p, 256, 16), False, p == 15)
-            ts(A("BX1"), PB(bg, 16, 32), 512.0, OP.is_ge, 7680.0, OP.mult)
+            ts(A("BX1"), PB(bb, 16, 32), 512.0, OP.is_ge, 7680.0, OP.mult)
             if nodes > 1024:
-                ts(A("BX2"), PB(bg, 16, 32), 1024.0, OP.is_ge, 8192.0, OP.mult)
+                ts(A("BX2"), PB(bb, 16, 32), 1024.0, OP.is_ge, 8192.0, OP.mult)
                 tt(A("BX1"), A("BX1"), A("BX2"), OP.add)
             tt(A("BX1"), A("BX1"), AD_, OP.subtract)
-            tt(A("DF", 16, 32), PB(bg, 0, 16), A("BX1"), OP.add)
+            tt(A("BX1"), PB(bb, 16, 32), A("BX1"), OP.add)
+            tt(A("DF", 16, 32), PB(bb, 32, 48), A("BX1"), OP.add)
             tt(A("DF", 0, 16), A("CO"), V_, OP.subtract)
         tt(A("ADD"), AD_, A("D12", 0, 16), OP.subtract)
         tt(A("CND", 0, 16), A("CO"), A("DUM"), OP.subtract)
         ts(A("ES"), A("E16"), -2048.0, OP.add)
-        act(A("EZ"), ("I", lzw, A("C16")), FN.Copy)
+        renew(1)
         mm(PB(1, 0, 256), A("LW2"), A("NN"), True, False)
-        ts(A("FG"), PB(0, 0, 256), 780.0, OP.is_gt)
-        mm(PB(1, 0, 256), A("SP"), A("FG"), False, True)
-        ts(A("OH"), PB(1, 0, 256), 0.0, OP.is_gt)
-        tt(A("M3", 0, 256), A("OH"), A("QKM"), OP.mult)
-        ts(A("M3", 512, 768), A("OH"), kc(1), OP.mult)
+        mm(PB(1, 0, 256), A("SPH"), A("ONE"), False, False)
+        act(A("FG"), PB(0, 0, 256), FN.Sign, bias=kc(7))
+        mm(PB(1, 0, 256), A("SPH"), A("FG"), False, True)
+        bh = nb()
+        OH = PB(bh, 0, 256)
+        act(OH, PB(1, 0, 256), FN.Relu)
+        tt(A("M3", 0, 256), OH, A("QKM"), OP.mult)
+        tt(A("M3", 256, 512), OH, A("ES"), OP.mult)
+        ts(A("M3", 512, 768), OH, kc(1), OP.mult)
         ts(A("OHC"), A("M3", 0, 256), 0.0, OP.not_equal)
-        tt(A("M3", 256, 512), A("OHC"), A("ES"), OP.mult)
         bk = nb()
         for h in range(2):
             mm(PB(bk, 8 * h, 8 * h + 8), A("M3", 128 * h, 128 * h + 128), A("GSEL"))
-        cp(A("KP"), PB(bk, 0, 16))
+        act(A("KP"), PB(bk, 0, 16), FN.Copy)
         act(A("KPN"), PB(bk, 0, 16), FN.Copy, scale=-1.0)
         po = conv("M3", 0, 768)
         MQ, ML, KL = PB(po, 0, 16), PB(po, 16, 32), PB(po, 32, 48)
@@ -609,7 +694,8 @@ def rank_program(g, core, T, topo):
         tt(A("LF2"), KL, A("NAQ"), OP.is_equal)
         tt(A("DN"), KL, A("ZE"), OP.is_equal)
         act(A("XQ"), ("I", A("X", 0, 4096), A("LU", 16, 32)), FN.Copy)
-        bx = 2
+        act(A("XL"), ("I", A("X", 0, 4096), A("LU", 0, 16)), FN.Copy)
+        bx = nb()
         mm(PB(bx, 0, 256), A("GEI"), A("OHC"))
         mm(PB(bx, 256, 512), A("IDB"), A("ONE"), True, False)
         mm(PB(bx, 256, 512), A("GEN"), A("OHC"), False, True)
@@ -628,24 +714,29 @@ def rank_program(g, core, T, topo):
                 else:
                     ts(A("EQ", 384 * q, 384 * q + 256), h0, A("KP", q, q + 1), OP.is_equal)
                     ts(A("EQ", 384 * q + 256, 384 * q + 384), h1, A("KP", 8 + q, 9 + q), OP.is_equal)
+        renew(0, 1)
         e0 = 768 * (2 - EQS)
         act(A("EQ", 1536 + e0, 3072), A("AEQ", e0, 1536), FN.Relu, scale=-1.0, bias=1.0)
         for q in range(8):
-            W, B_ = A("W0", 128 * q, 128 * q + 128), A("BIG", 128 * q, 128 * q + 128)
+            W, B_ = A("W0", 112 - 16 * q, 240 - 16 * q), A("BIG", 112 - 16 * q, 240 - 16 * q)
             mm(PB(0, 0, 128), W, A("EQ", 384 * q, 384 * q + 128), q == 0, q == 7)
             mm(PB(1, 0, 128), B_, A("EQ", 384 * q + 128, 384 * q + 256), q == 0, False)
             mm(PB(1, 0, 128), W, A("EQ", 384 * q + 256, 384 * q + 384), False, q == 7)
         tt(LF, A("LF2"), A("LF1"), OP.add)
         ts(A("RW"), A("LQ"), 15, OP.bitwise_and)
-        tt(TWO, A("RW", 0, 16), A("RW", 16, 32), OP.not_equal)
-        tt(A("XA"), ("I", A("X", 0, 4096), A("LU", 0, 16)), A("XQ"), OP.add)
+        tt(A("TW0"), A("RW", 0, 16), A("RW", 16, 32), OP.not_equal)
+        tt(TWO, A("TW0"), CC, OP.mult)
+        bsum = nb()
+        mm(PB(bsum, 0, 256), A("IDB"), A("XQ"), True, False)
+        mm(PB(bsum, 0, 256), A("IDB"), A("XL"), False, True)
         tt(A("FL", 0, 128), PB(0, 0, 128), A("WB2"), OP.is_lt)
         tt(A("FL", 128, 256), PB(1, 0, 128), A("WB2"), OP.is_lt)
         bf = conv("FL", 0, 256)
-        ts(A("XB"), A("XA"), 1, OP.arith_shift_right)
+        ts(A("XB"), PB(bsum, 0, 256), 0.5, OP.mult, -0.25, OP.add)
         tt(A("XS"), A("LQ", 16, 32), A("DX"), OP.subtract)
-        tt(A("XF"), PB(bf, 0, 16), CC, OP.min)
+        ts(A("XF"), MQ, 0.0, OP.not_equal, 0.0625, OP.mult)
         tt(A("XS"), A("XS"), A("XF"), OP.mult)
+        tt(A("XS"), PB(bf, 0, 16), A("XS"), OP.mult)
         tt(A("XS"), A("XS"), A("DX"), OP.add)
         cp(A("XSU"), A("XS"))
         cp(("I", A("X"), A("XSU")), A("XB"))
@@ -681,6 +772,7 @@ def rank_program(g, core, T, topo):
             mm(PB(ba, 0, 16), A("NID"), LF, False, False)
             mm(PB(ba, 0, 16), A("NID"), A("SV"), False, True)
             act(A("AL"), PB(ba, 0, 16), FN.Copy)
+            tt(A("ALV"), PB(ba, 0, 16), A("VMD"), OP.mult)
             act(A("AL5"), PB(ba, 0, 16), FN.Identity, scale=512.0, bias=-1.0)
             tt(A("KX"), A("LCX"), A("DN"), OP.mult)
             tt(A("KX"), A("KX"), A("LAB", 16, 32), OP.add)
@@ -710,15 +802,16 @@ def rank_program(g, core, T, topo):
             cp(("I", A("BB"), A("CLU")), A("NDD"))
 
     def travel(r):
+        renew(2)
         expand(2, "NAH", 16)
         ts(A("OHA"), PB(2, 0, 256), kc(1), OP.is_equal)
         b = nb()
         mm(PB(b, 0, 256), A("GEI"), A("OHA"))
-        tt(A("T1"), PB(b, 0, 256), A("HD"), OP.mult)
-        tt(A("T2"), A("T1"), A("QTF"), OP.add)
+        tt(PB(b, 0, 256), PB(b, 0, 256), A("HD"), OP.mult)
+        tt(PB(b, 0, 256), PB(b, 0, 256), A("QI"), OP.add)
         lo = 256 * r
         qx = A("QX", lo, lo + 256)
-        cp(qx, A("T2"))
+        cp(qx, PB(b, 0, 256))
         cp(A("QN", lo, lo + 32), A("QX", lo, lo + 32))
         tr, free = [], {}
         dsts = [(e, T.cores[(rank + e) % N]) for e in range(1, N)]
@@ -731,7 +824,7 @@ def rank_program(g, core, T, topo):
             tr.append(RemoteDMATransfer(dst_ids=[DstId(rid=rid, pnc=pid)], dma_engine_mask=sum(1 << x for x in es),
                                         remote_sem=T.sem["arr%d" % r], src=T.QX[:, c0:c0 + 32], dst=T.QN[:, c0:c0 + 32], alu_op=0))
         do("G", lambda e: e.remote_dma_fused(tr, local_sem=T.sem["loc"]), [A("QN", lo + 32, lo + 256)], [qx],
-           sem="arr%d" % r, inc=len(used), cost=1500.0, lat=5000.0)
+           sem="arr%d" % r, inc=len(used), cost=(1500.0, 0, 0, 0, 0, 0), lat=5000.0)
 
     for s in range(3):
         step(0, s)
@@ -765,7 +858,7 @@ def rank_program(g, core, T, topo):
     store("Y", "yr", T.yr[:, :], A("YR"))
     if not _ORDER:
         _ORDER.append(order())
-    for i in _ORDER[0]:
-        issue(*nodes[i])
+    for i in _ORDER[0][0]:
+        issue(*nodes[i][:6])
     for sname in sorted(cnt):
         need("G", sname, cnt[sname])

import math
import numpy as np
from concourse.mybir import dt, AluOpType, ActivationFunctionType
from concourse.bass import DstId, RemoteDMATransfer

F, H, BFL, I32, U16 = "float32", "float16", "bfloat16", "int32", "uint16"
CFW = 16384 + 512 + 8192
_S = {
    "X": (4352, BFL), "LZ": (1792, F), "CF": (CFW, F), "BB": (2048, F), "OC0": (1792, BFL), "OC1": (1792, BFL),
    "REQ": (256, I32), "CHI": (512, I32), "EDG": (512, I32), "CHH": (512, H),
    "QX": (512, U16), "QN": (512, U16), "QI": (256, I32), "Q16": (256, U16),
    "QZ": (256, F), "QK": (256, H), "QK0": (256, H), "QS": (256, H), "QR": (256, H), "QTI": (256, I32), "QTF": (256, F),
    "HD": (256, F), "HI": (256, I32), "HM": (256, F),
    "IPI": (16, I32), "KPI": (16, I32), "KC": (8, F), "K0": (1, F), "ROWX": (128, F), "COLM": (128, F), "DIFF": (128, F), "COLX": (128, BFL),
    "ONE": (256, BFL), "GB": (1024, BFL), "ZG": (240, F), "W0": (240, BFL), "BIG": (240, BFL), "GSEL": (8, BFL),
    "BD2": (256, BFL), "SELA": (2048, BFL), "SELR": (2048, BFL), "IDB": (128, BFL), "NID": (128, BFL),
    "LST": (128, BFL), "GEI": (128, BFL), "LW2": (128, BFL), "SP": (128, BFL), "SHF": (128, BFL),
    "EXT": (152, F), "WO2": (16, F), "WB2": (128, F), "ND": (512, F), "NDD": (512, F), "OV": (256, BFL),
    "LDR": (16, F), "LDC": (16, F), "LDB": (16, F), "LDQ": (16, F), "LDL": (16, F), "ADR": (16, F), "KPN": (16, F),
    "LI": (16, F), "DUM": (16, F), "DX": (16, F), "D12": (32, F), "NBD": (32, F), "DCN": (32, F), "CND": (32, F), "J16": (16, F),
    "QD": (4096, BFL), "D4": (4096, BFL), "ED": (2048, BFL), "EQ": (3072, BFL), "AEQ": (1536, BFL),
    "OHA": (256, BFL), "R1": (256, BFL), "R2": (256, BFL), "EZ": (256, F), "E16": (256, U16), "ES": (256, H), "G": (256, H),
    "RM": (256, H), "QZA": (256, F), "QG": (256, H), "QKM": (256, H), "NN": (256, BFL), "KLB": (256, BFL), "CT": (768, H),
    "FG": (256, BFL), "OH": (256, H), "M3": (768, H), "OHC": (256, H), "T1": (256, F), "T2": (256, F), "T3": (256, F), "T4": (256, F),
    "FR": (256, F), "AB": (512, BFL), "ABT": (512, BFL), "TM": (256, BFL), "RB": (384, BFL), "OG": (512, BFL), "BG": (256, H),
    "FL": (256, H), "XQ": (256, BFL), "XL": (256, BFL), "XB": (256, I32), "KP": (16, F), "YR": (256, F),
    "ST": (48, F), "DF": (48, F), "Q3": (48, F), "VA16": (32, U16), "C16": (16, U16), "CO": (16, F), "NAH": (16, BFL),
    "FTB": (64, BFL), "GEN": (128, BFL), "TW0": (16, F), "SPH": (128, BFL), "OHT": (256, BFL), "VMD": (16, F), "ALV": (16, F), "AL5": (16, F), "LF2": (16, F), "AL": (16, BFL), "AC": (16, F), "AT2": (16, F), "ACT": (16, F), "ATH": (16, BFL), "LF1": (16, F), "HC": (16, F), "NOC": (16, F),
    "OLI": (16, F), "OL16": (16, U16), "CKH": (16, BFL), "NAQ": (16, F), "ZE": (16, F), "LAB": (32, F), "LCX": (16, F), "LD": (16, F),
    "ADD": (16, F), "BX1": (16, F), "BX2": (16, F), "FUL": (16, F), "CC": (32, F), "FT": (32, F), "LF": (16, F), "DN": (16, F),
    "SV": (16, BFL), "LQ": (32, I32), "LU": (32, U16), "RW": (32, I32), "RWF": (32, F), "A12": (32, F), "A12U": (32, U16), "LQT": (16, F),
    "CL": (32, F), "CLU": (32, U16), "XF": (16, F), "XS": (16, F), "XSU": (16, U16), "KX": (16, F), "KXI": (16, I32), "KHI": (32, I32),
    "KH": (32, H), "LFT": (32, H),
}
SCRATCH = {"P%d" % b: ("psum", [128, 512], "float32") for b in range(8)}
_PLACE = {}
_SMALL = {F: "SMF", H: "SMH", I32: "SMI", U16: "SMU", BFL: "SMB"}
_fill = {}
for _n in _S:
    if _S[_n][0] <= 64:
        _b = _SMALL[_S[_n][1]]
        _PLACE[_n] = (_b, _fill.get(_b, 0))
        _fill[_b] = _fill.get(_b, 0) + (_S[_n][0] + 15) // 16 * 16
        SCRATCH[_b] = ("sbuf", [128, _fill[_b]], _S[_n][1])
    else:
        _PLACE[_n] = (_n, 0)
        SCRATCH[_n] = ("sbuf", [128, _S[_n][0]], _S[_n][1])
_LOADS = ["req", "child", "edge", "d0", "d1", "yd", "ye0", "ye1", "yr"]
SEMAPHORES = ["sV", "sS", "sT", "sG", "arr0", "arr1", "loc"] + ["l_" + n for n in _LOADS]

OP, FN = AluOpType, ActivationFunctionType


def A(name, c0=0, c1=None, st=1):
    b, o = _PLACE[name]
    return (b, o + c0, o + (_S[name][0] if c1 is None else c1), st)


WAKE, SLACK = 70.0, 60.0
SETS = [(5, 0.9, 1.56, 3.8, 0.75, 70, 182.0), (0, 0.85, 1.2, 2.2, 0.6, 40, 150.0), (0, 0.9, 2.0, 5.5, 0.65, 60, 200.0),
        (0, 0.9, 1.5, 3.5, 0.45, 40, 165.0), (10, 0.85, 1.5, 3.8, 0.6, 130, 190.0)]
PASSES, SEEDS, KEPT = 6, (), []
_ORDER = []
CFV = 17
EQS = 2
ONV = 4


def is_psum(name):
    return name[0] == "P" and name[1:].isdigit()


def rank_program(g, core, T, topo):
    rank = T.rank_of(core)
    if rank is None:
        return
    N = len(T.cores)
    queues = {"V": g.vector, "S": g.scalar, "T": g.tensor, "G": g, "Y": g.sync}
    cnt, clock, hist = {}, {}, {}
    known = {q: {} for q in queues}

    def real(x):
        return (_ORDER[0][1][x[0]],) + x[1:] if is_psum(x[0]) else x

    def ap(x):
        x = real(x)
        return T[x[0]][:, x[1]:x[2]:x[3]] if x[3] != 1 else T[x[0]][:, x[1]:x[2]]

    def need(q, src, n):
        if known[q].get(src, 0) >= n:
            return
        queues[q].wait_ge(T.sem[src], n)
        for k, v in clock.get((src, n), {}).items():
            if known[q].get(k, 0) < v:
                known[q][k] = v
        known[q][src] = n

    nodes = []

    def price(k, z):
        a = SETS[z]
        return k[0] + k[1] * a[0] + a[1] * (k[2] + k[3] * a[2] + k[4] * a[3]) + k[5] * a[4]

    def do(q, call, outs, ins, sem=None, inc=1, cost=(100.0, 0, 0, 0, 0, 0), lat=0.0):
        nodes.append((q, call, outs, ins, sem, inc, price(cost, 0), lat, cost))

    def order():
        n = len(nodes)
        succ, npre = [[] for _ in range(n)], [0] * n
        last = {}
        for i, (q, call, outs, ins, sem, inc, cost, lat, parts_) in enumerate(nodes):
            pre = set()
            for acc, w in [(x, False) for x in ins] + [(x, True) for x in outs]:
                h = last.setdefault(acc[0], [])
                ps = is_psum(acc[0])
                for (lo, hi, hw, j) in h:
                    if j != i and (ps or (lo < acc[2] and acc[1] < hi and (w or hw))):
                        pre.add(j)
                if ps:
                    h[:] = [(0, 512, True, i)]
                else:
                    if w and acc[3] == 1:
                        h[:] = [e for e in h if not (acc[1] <= e[0] and e[1] <= acc[2])]
                    h.append((acc[1], acc[2], w, i))
            for j in pre:
                succ[j].append(i)
            npre[i] = len(pre)
        prio = [0.0] * n
        for i in range(n - 1, -1, -1):
            prio[i] = nodes[i][6] + nodes[i][7] + max([prio[j] + (0 if nodes[j][0] == "T" == nodes[i][0] else WAKE) for j in succ[i]], default=0.0)
        pred = [[] for _ in range(n)]
        for i in range(n):
            for j in succ[i]:
                pred[j].append(i)

        banks = [sorted(set(x[0] for x in nd[2] + nd[3] if is_psum(x[0]))) for nd in nodes]
        uses = {}
        for bs in banks:
            for b in bs:
                uses[b] = uses.get(b, 0) + 1

        def run(follow, left, prio, latency, limited):
            left, at, end = list(left), [0.0] * n, [0.0] * n
            ready, free, res = {q: [] for q in queues}, {q: 0.0 for q in queues}, []
            idle, has, rest = {"P%d" % b: 0.0 for b in range(8)}, {}, dict(uses)
            for i in range(n):
                if left[i] == 0:
                    ready[nodes[i][0]].append(i)

            def when(i):
                if limited:
                    new = [b for b in banks[i] if b not in has]
                    if new:
                        if len(idle) < len(new):
                            return 1e12
                        return max(at[i], sorted(idle.values())[len(new) - 1] + WAKE)
                return at[i]

            while len(res) < n:
                best = None
                for q in queues:
                    if ready[q]:
                        t = max(free[q], min(when(i) for i in ready[q]))
                        if best is None or t < best[0]:
                            best = (t, q)
                t, q = best
                if t >= 1e12:
                    return 1e12, res, end, has
                i = max((i for i in ready[q] if when(i) <= t + SLACK), key=lambda i: (prio[i] - max(0.0, when(i) - t), -i))
                t = max(t, when(i))
                ready[q].remove(i)
                res.append(i)
                free[q] = end[i] = t + nodes[i][6]
                if limited:
                    for b in banks[i]:
                        if b not in has:
                            has[b] = min(idle, key=lambda z: (idle[z], z))
                            del idle[has[b]]
                        rest[b] -= 1
                        if rest[b] == 0:
                            idle[has[b]] = end[i]
                for j in follow[i]:
                    at[j] = max(at[j], end[i] + (nodes[i][7] if latency else 0.0) + (0 if nodes[j][0] == "T" == q else WAKE))
                    left[j] -= 1
                    if left[j] == 0:
                        ready[nodes[j][0]].append(j)
            return max(end), res, end, has

        def length(res, has, z):
            wake = SETS[z][5]
            end, qend, bend, opened = [0.0] * n, {q: 0.0 for q in queues}, {}, {}
            for i in res:
                nd = nodes[i]
                q, t = nd[0], qend[nd[0]]
                for j in pred[i]:
                    u = end[j] + nodes[j][7] + (0 if q == "T" == nodes[j][0] else wake)
                    if u > t:
                        t = u
                for b in banks[i]:
                    if b not in opened:
                        opened[b] = True
                        t = max(t, bend.get(has[b], 0.0) + wake)
                c = COSTS[z][i]
                end[i] = qend[q] = t + c
                for b in banks[i]:
                    bend[has[b]] = max(bend.get(has[b], 0.0), t + c)
            return max(end)

        COSTS = [[nd[6] if z == 0 else price(nd[8], z) for nd in nodes] for z in range(len(SETS))]

        def score(res, has):
            return sum(length(res, has, z) / SETS[z][6] for z in range(len(SETS)))

        best = None
        for k in range(PASSES + len(SEEDS)):
            if k >= PASSES:
                rng = np.random.default_rng(SEEDS[k - PASSES])
                z = rng.normal(0.0, 1.0, n) * (rng.random(n) < rng.choice([0.02, 0.1, 0.5])) * rng.choice([300.0, 1500.0])
                prio = [a + float(b) for a, b in zip(best[3], z)]
            span, res, end, has = run(succ, npre, prio, True, True)
            if span < 1e12:
                sc = score(res, has)
                if best is None or sc < best[0]:
                    best = (sc, res, has, prio)
                    if k >= PASSES:
                        KEPT.append((sc, SEEDS[k - PASSES]))
            if k < PASSES:
                if span >= 1e12:
                    end = run(succ, npre, prio, True, False)[2]
                prio = run(pred, [len(x) for x in succ], end, False, False)[2]
        return best[1], best[2]

    def issue(q, call, outs, ins, sem=None, inc=1):
        src = sem or "s" + q
        outs, ins = [real(x) for x in outs], [real(x) for x in ins]
        deps = {}
        for acc, w in [(x, False) for x in ins] + [(x, True) for x in outs]:
            ps = is_psum(acc[0])
            for (lo, hi, hw, hq, hs, hn) in hist.get(acc[0], []):
                same = hq == q and sem is None and hs == "s" + q
                if ps and not same:
                    hit = True
                else:
                    hit = lo < acc[2] and acc[1] < hi and (w or hw)
                    if same and q == "T":
                        hit = False
                if hit:
                    deps[hs] = max(deps.get(hs, 0), hn)
        for s in sorted(deps, key=lambda s: s == src):
            need(q, s, deps[s])
        ins_ = call(queues[q])
        if sem in ("arr0", "arr1"):
            cnt[sem] = inc
            cnt["loc"] = cnt.get("loc", 0) + inc
            hist.setdefault("QN", []).append((outs[0][1], outs[0][2], True, "R", sem, inc))
            return
        cnt[src] = cnt.get(src, 0) + inc
        n = cnt[src]
        ins_.then_inc(T.sem[src], inc)
        snap = dict(known[q])
        clock[(src, n)] = snap
        for acc, w in [(x, False) for x in ins] + [(x, True) for x in outs]:
            h = hist.setdefault(acc[0], [])
            ps = is_psum(acc[0])
            if ps:
                h[:] = [e for e in h if e[3] == q and not (acc[1] <= e[0] and e[1] <= acc[2])]
            elif w and acc[3] == 1:
                h[:] = [e for e in h if not (acc[1] <= e[0] and e[1] <= acc[2])]
            elif not w:
                h[:] = [e for e in h if not (not e[2] and e[4] == src and acc[1] <= e[0] and e[1] <= acc[2])]
            h.append((acc[1], acc[2], w, q, src, n))

    def iap(x):
        return ap(x[1]).indirect(ap(x[2])) if x[0] == "I" else ap(x)

    def parts(*xs):
        r = []
        for x in xs:
            if isinstance(x, tuple):
                r += [x[1], x[2]] if x[0] == "I" else [x]
        return r

    def oparts(out, ins):
        return ([out[1]], ins + [out[2]]) if out[0] == "I" else ([out], ins)

    def wid(x):
        return 16 * (x[2][2] - x[2][1]) if x[0] == "I" else (x[2] - x[1] + x[3] - 1) // x[3]

    def vcost(out, *xs):
        n = wid(out)
        if out[0] == "I":
            return (50, 0, 0, 0, n, 0)
        elif any(x[0] == "I" for x in xs):
            return (50, 0, 0, n, 0, 0)
        elif len(xs) == 2:
            c = n if any(is_psum(x[0]) for x in xs) else 2 * n
        else:
            c = n * (0.5 if all(not is_psum(x[0]) and SCRATCH[x[0]][2] in (H, BFL, U16) for x in (out, xs[0])) else 1)
        return (0, 1, max(64, c), 0, 0, 0)

    def tt(out, a, b, op):
        o, i = oparts(out, parts(a, b))
        do("V", lambda e: e.tensor_tensor(iap(out), iap(a), iap(b), op), o, i, cost=vcost(out, a, b))

    def ts(out, a, s1, op0, s2=None, op1=None):
        o, i = oparts(out, parts(a, s1, s2))
        v1 = ap(s1) if isinstance(s1, tuple) else s1
        v2 = ap(s2) if isinstance(s2, tuple) else s2
        if op1 is None:
            do("V", lambda e: e.tensor_scalar(iap(out), iap(a), v1, None, op0), o, i, cost=vcost(out, a))
        else:
            do("V", lambda e: e.tensor_scalar(iap(out), iap(a), v1, v2, op0, op1), o, i, cost=vcost(out, a))

    def cp(out, a):
        o, i = oparts(out, parts(a))
        do("V", lambda e: e.tensor_copy(iap(out), iap(a)), o, i, cost=vcost(out, a))

    def fill(out, c):
        do("V", lambda e: e.memset(ap(out), c), [out], [], cost=(0, 1, max(64, wid(out)), 0, 0, 0))

    def act(out, a, fn, scale=1.0, bias=0.0):
        i = parts(a, scale, bias)
        sc = ap(scale) if isinstance(scale, tuple) else scale
        bi = ap(bias) if isinstance(bias, tuple) else bias
        do("S", lambda e: e.activation(iap(out), iap(a), fn, bias=bi, scale=sc), [out], i,
           cost=(65, 0, 0, wid(out), 0, 0) if a[0] == "I" else (1600 if fn == FN.Exp else 0, 1, max(64, wid(out)), 0, 0, 0))

    def mm(out, lhsT, rhs, start=True, stop=True):
        do("T", lambda e: e.matmul(ap(out), ap(lhsT), ap(rhs), start, stop), [out], [lhsT, rhs], cost=(0, 0, 0, 0, 0, max(64, wid(rhs))))

    def iota(out, pattern, base, cm):
        c = (160 + 2.08 * wid(out), 0, 0, 0, 0, 0)
        if SCRATCH[out[0]][2] == I32:
            do("G", lambda e: e.iota(ap(out), pattern, base, cm), [out], [], cost=c)
        else:
            do("G", lambda e: e.iota(ap(out), pattern, base, cm, allow_small_or_imprecise_dtypes=True), [out], [], cost=c)

    def load(q, name, buf, src):
        do(q, lambda e: e.dma_start(ap(buf), src), [buf], [], sem="l_" + name, inc=16, lat=2000 + 2.0 * wid(buf))

    def store(q, name, dst, buf):
        do(q, lambda e: e.dma_start(dst, ap(buf)), [], [buf], sem="l_" + name, inc=16, lat=2000 + 2.0 * wid(buf))

    VL16, AD16 = A("VA16", 0, 16), A("VA16", 16, 32)
    rot = [7]

    def nb():
        rot[0] += 1
        return rot[0]

    cur = {}

    def renew(*bs):
        for b in bs:
            cur[b] = nb()

    def PB(b, c0, c1, st=1):
        return ("P%d" % cur.get(b, b), c0, c1, st)

    def SELA(p):
        return A("SELA", 128 * p, 128 * p + 128)

    def SELR(p):
        return A("SELR", 128 * p, 128 * p + 128)

    def conv(name, c0, w):
        b = nb()
        for p in range(16):
            mm(PB(b, 0, w // 16), SELA(p), A(name, c0 + p, c0 + w, 16), p == 0, p == 15)
        return b

    def expand(b, name, w):
        for q in range(16):
            mm(PB(b, q, 16 * w, 16), SELR(q), A(name, 0, w))

    def kc(j):
        return A("KC", j, j + 1)

    load("Y", "req", A("REQ"), T.req[:, :])
    load("S", "child", A("CHI"), T.child[:, :])
    load("Y", "d0", A("X", 0, 2048), T.desc[:, 0:2048])
    load("S", "edge", A("EDG"), T.edge[:, :])
    load("Y", "d1", A("X", 2048, 4096), T.desc[:, 2048:4096])
    iota(A("IPI"), [[0, 16]], 0, 1)
    iota(A("ROWX"), [[-16, 8], [0, 16]], 0, 1)
    iota(A("COLM"), [[0, 8], [1, 16]], 1, 0)
    iota(A("DIFF"), [[1, 128]], 0, -1)
    iota(A("J16"), [[16, 16]], 0, 0)
    iota(A("EXT", 0, 16), [[0, 2], [16, 8]], 0, 0)
    iota(A("EXT", 16, 144), [[1, 128]], 0, 0)
    iota(A("EXT", 144, 152), [[0, 8]], 0, 1)
    iota(A("OC0"), [[0, 1792]], 0, 0)
    iota(A("OC1"), [[0, 1792]], 0, 0)
    iota(A("OV"), [[1, 256]], 1, 0)
    iota(A("GB"), [[-16, 8], [0, 128]], 0, 1)
    iota(A("ZG"), [[1, 15], [0, 16]], -7, 0)
    iota(A("ND", 0, 256), [[2, 256]], 512, 0)
    iota(A("ND", 256, 512), [[2, 256]], 513, 0)
    iota(A("CF", 8192, 16896), [[0, 8704]], 0, 0)
    iota(A("BB"), [[1, 2048]], 0, 0)
    iota(A("LZ", 512, 1792), [[0, 1280]], 0, 0)

    ts(A("KPI"), A("IPI"), 15, OP.bitwise_and)
    cp(kc(0), A("KPI", 0, 1))
    ts(kc(1), A("KPI", 0, 1), -1.0, OP.mult, 16.0, OP.add)
    ts(kc(2), A("KPI", 0, 1), -8192.0, OP.mult, 131072.0, OP.add)
    ts(kc(3), A("KPI", 0, 1), 0.0, OP.is_gt)
    ts(A("K0"), A("KPI", 0, 1), 0.0, OP.is_equal)
    ts(A("BD2", 0, 128), A("ROWX"), kc(0), OP.is_equal)
    tt(A("COLX"), A("BD2", 0, 128), A("COLM"), OP.mult)
    for p in range(16):
        ts(SELA(p), A("COLX"), float(p + 1), OP.is_equal)

    def requests(r):
        src = "REQ" if r == 0 else "QN"
        s0 = A(src, 0, 256)
        ts(A("QTF"), s0, 2048.0, OP.is_ge, -2048.0, OP.add)
        if r == 0:
            cp(A("QI"), A("REQ"))
        else:
            cp(A("QI"), s0)
        tt(A("QK"), A("QTF"), A("QI"), OP.add)
        ts(A("QK0"), A("QK"), A("K0"), OP.mult)
        b = conv("QK0", 0, 256)
        cp(A("Q16"), s0)
        ts(A("LDR"), PB(b, 0, 16), 0.0, OP.is_gt, -2048.0, OP.add)
        tt(A("LQ", 0, 16), PB(b, 0, 16), A("LDR"), OP.subtract)
        ts(A("KXI"), A("LQ", 0, 16), 4, OP.arith_shift_right)
        ts(A("LQ", 16, 32), A("LQ", 0, 16), 15, OP.bitwise_and)
        cp(VL16, A("KXI"))
        cp(A("ST", 0, 16), A("KXI"))

    def requests2(r):
        ts(A("QTI"), A("QI"), 15, OP.bitwise_and)
        ts(A("QR"), A("QTI"), 512.0, OP.mult)
        ts(A("QZ"), A("QI"), -1.0, OP.mult, 4095.0, OP.add)
        ts(A("QG"), A("QK"), kc(3), OP.mult)

    def hashes(r):
        ts(A("QS"), A("QI"), -2048.0, OP.add)
        b = nb()
        mm(PB(b, 0, 256), A("SHF"), A("QS"))
        act(PB(b, 256, 512), PB(b, 0, 256), FN.Identity, bias=2048.0)
        tt(A("HI"), PB(b, 256, 512), A("QI"), OP.mult)
        ts(A("HI"), A("HI"), 5, OP.logical_shift_right, 4095, OP.bitwise_and)
        b = nb()
        ts(PB(b, 0, 256), A("HI"), 4095.0, OP.is_lt, kc(3), OP.mult)
        tt(PB(b, 0, 256), PB(b, 0, 256), A("HI"), OP.mult)
        ts(A("HM"), A("QI"), kc(3), OP.mult)
        tt(A("HD"), PB(b, 0, 256), A("HM"), OP.subtract)

    def queries(c):
        act(A("QD", 1024 * c, 1024 * c + 1024), ("I", A("X", 0, 4096), A("Q16", 64 * c, 64 * c + 64)), FN.Copy)

    def digits():
        ts(A("KHI", 0, 16), A("KXI"), 4, OP.arith_shift_right)
        ts(A("KHI", 16, 32), A("KXI"), 15, OP.bitwise_and)
        cp(A("KH"), A("KHI"))

    requests(0)
    digits()
    ts(A("RWF", 0, 16), A("LQ", 16, 32), 512.0, OP.mult)
    for q in range(16):
        ts(SELR(q), A("ROWX"), float(q), OP.is_equal)
    cp(A("NAH"), A("LQ", 16, 32))
    renew(2)
    expand(2, "NAH", 16)
    ts(A("RM"), PB(2, 0, 256), kc(0), OP.is_equal)
    ts(A("IDB"), A("DIFF"), 0.0, OP.is_equal)
    cp(A("CHH"), A("CHI"))
    ts(A("LZ", 0, 512), A("EDG"), -1.0, OP.mult, 4095.0, OP.add)
    for t in range(16):
        b = nb()
        mm(PB(b, 0, 512), SELR(t), A("CHH"))
        if t % CFV == CFV - 1:
            cp(A("CF", 512 * t, 512 * t + 512), PB(b, 0, 512))
        else:
            act(A("CF", 512 * t, 512 * t + 512), PB(b, 0, 512), FN.Copy)
    cp(A("LDC"), A("KPI"))
    tt(A("LI"), A("J16"), A("LDC"), OP.add)
    tt(A("EXT", 0, 16), A("EXT", 0, 16), A("LDC"), OP.add)
    ln = math.log(2.5)
    ts(A("EXT", 0, 144), A("EXT", 0, 144), -ln, OP.mult, 64 * ln + math.log(2.0), OP.add)
    ts(A("EXT", 144, 145), A("EXT", 144, 145), -ln, OP.mult, 64 * ln, OP.add)
    ts(A("EXT", 145, 146), A("EXT", 145, 146), -ln / 2, OP.mult, 32 * ln, OP.add)
    act(A("WO2"), A("EXT", 0, 16), FN.Exp)
    act(A("WB2"), A("EXT", 16, 144), FN.Exp)
    act(A("KC", 4, 6), A("EXT", 144, 146), FN.Exp)
    cp(A("BD2", 128, 256), A("BD2", 0, 128))
    ts(A("NID"), A("IDB"), -1.0, OP.mult)
    ts(A("LST"), A("DIFF"), 0.0, OP.is_gt)
    tt(A("LST"), A("LST"), A("BD2", 0, 128), OP.mult)
    tt(A("GEI"), A("LST"), A("IDB"), OP.add)
    ts(A("GEN"), A("GEI"), -1.0, OP.mult)
    ts(A("LW2"), A("LST"), -2.0, OP.mult)
    tt(A("SP"), A("IDB"), A("LW2"), OP.add)
    ts(A("SPH"), A("SP"), 0.5, OP.mult)
    fill(kc(7), -780.5)
    ts(kc(6), kc(1), -1.0, OP.mult)
    ts(A("SHF"), A("DIFF"), 1.0, OP.is_equal)
    ts(A("DUM"), A("LI"), 1536.0, OP.add)
    ts(A("DX"), A("LI"), 4096.0, OP.add)
    ts(A("D12", 0, 16), A("LI"), 16384.0, OP.add)
    ts(A("D12", 16, 32), A("LI"), 16640.0, OP.add)
    cp(A("DCN", 0, 16), A("DUM"))
    ts(A("DCN", 16, 32), A("LI"), 1792.0, OP.add)
    ts(A("GB"), A("GB"), kc(0), OP.is_equal)
    cp(A("GSEL"), A("GB", 0, 1024, 128))
    ts(A("W0"), A("ZG"), 0.0, OP.is_equal, kc(4), OP.mult)
    ts(A("BIG"), A("ZG"), 0.0, OP.is_equal, 1e28, OP.mult)
    fill(A("ONE"), 1.0)
    requests2(0)
    hashes(0)
    for c in range(4):
        queries(c)
    for z in range(16896, CFW, 1024):
        iota(A("CF", z, z + 1024), [[0, 1024]], 0, 0)

    def step(r, s):
        first, end, final = s == 0, s == 2, r == 1 and s == 2
        stamp = 1 + 3 * r + s
        nbase = 512 + 512 * r
        boff = 7680.0 if r == 0 else 15872.0
        nodes = 512 + 512 * r if first else 1024 + 512 * r
        lzw = A("LZ", 0, nodes)
        V_, AD_, NA_ = A("ST", 0, 16), A("ST", 16, 32), A("ST", 32, 48)
        oha = "OHA0" if first else "OHA"
        qza = "QZ" if first else "QZA"
        if first:
            fill(NA_, 16.0)
            fill(A("AL"), 1.0)
            tt(A("ALV"), V_, A("DUM"), OP.subtract)
            ts(A("NBD", 0, 16), A("LI"), 2.0, OP.mult, nbase + boff, OP.add)
            tt(A("NBD", 0, 16), A("NBD", 0, 16), A("D12", 0, 16), OP.subtract)
            ts(A("NBD", 16, 32), A("NBD", 0, 16), -256.0, OP.add)
            ts(A("CND", 16, 32), A("LI"), 2.0, OP.mult, float(nbase - 1792), OP.add)
            tt(A("CND", 16, 32), A("CND", 16, 32), A("LI"), OP.subtract)
            cp(A("NDD", 0, 256), A("ND", 0, 256))
        if r == 0 and first:
            tt(AD_, V_, A("RWF", 0, 16), OP.add)
            tt(A("G"), ("I", A("CHI"), VL16), A("RM"), OP.mult)
            b = conv("G", 0, 256)
            ts(A("C16"), PB(b, 0, 16), 1.0, OP.mult)
            act(A("CO"), PB(b, 0, 16), FN.Copy)
        else:
            cp(A("G"), ("I", A("CF", 0, 16896 if r == 0 else CFW), AD16))
            b = conv("G", 0, 256)
            ts(A("C16"), PB(b, 0, 16), 0.0625, OP.mult)
            act(A("CO"), PB(b, 0, 16), FN.Copy, scale=0.0625)
        expand(b4 := nb(), "KH", 32)
        ts(A("AB"), PB(b4, 0, 512), kc(0), OP.is_equal)
        ts(A("E16"), ("I", lzw, A("C16")), -1.0, OP.mult, 4095.0, OP.add)
        b = nb()
        for h in range(4):
            mm(PB(b, 128 * h, 128 * h + 128), A("AB", 128 * h, 128 * h + 128), A("IDB"))
        act(A("ABT"), PB(b, 0, 512), FN.Copy, scale=kc(5))
        act(A("EZ"), ("I", lzw, A("C16")), FN.Copy)
        act(A("R2"), A("EZ"), FN.Relu, scale=-8192.0, bias=8192.0)
        if not first:
            renew(2)
            expand(2, "NAH", 16)
            act(A("R1"), PB(2, 0, 256), FN.Relu, scale=-8192.0, bias=kc(2))
            act(A("OHT"), PB(2, 0, 256), FN.Abs, bias=kc(6))
            act(A("OHA"), A("OHT"), FN.Relu, scale=-1.0, bias=1.0)
            b = nb()
            mm(PB(b, 0, 256), A("GEI"), A("OHA"))
            mm(PB(b, 256, 512), A("LST"), A("OHA"))
            tt(A("QG"), PB(b, 256, 512), A("QK"), OP.mult)
            tt(A("QZA"), PB(b, 0, 256), A("QZ"), OP.mult)
        b = nb()
        for h in range(2):
            mm(PB(b, 128 * h, 128 * h + 128), A("ABT", 128 * h, 128 * h + 128), A("ABT", 256 + 128 * h, 384 + 128 * h))

        def dist(c):
            w = slice(64 * c, 64 * c + 64)
            lo, hi = 1024 * c, 1024 * c + 1024
            desc = ("I", A("X", 0, 4096), A("E16", w.start, w.stop))
            if c < ONV:
                tt(A("D4", lo, hi), desc, A("QD", lo, hi), OP.subtract)
                act(A("D4", lo, hi), A("D4", lo, hi), FN.Abs)
            else:
                act(A("ED", lo % 2048, lo % 2048 + 1024), desc, FN.Copy)
                for z in (0, 512):
                    bz = nb()
                    mm(PB(bz, 0, 512), A("IDB"), A("ED", lo % 2048 + z, lo % 2048 + z + 512), True, False)
                    mm(PB(bz, 0, 512), A("NID"), A("QD", lo + z, lo + z + 512), False, True)
                    act(A("D4", lo + z, lo + z + 512), PB(bz, 0, 512), FN.Abs)
            o = PB(0, w.start, w.stop)
            mm(o, A("NID"), A("R2", w.start, w.stop), True, False)
            if not first:
                mm(o, A("NID"), A("R1", w.start, w.stop), False, False)
            for k in range(16):
                mm(o, A("SELA", 128 * k, 128 * k + 128), A("D4", lo + k, hi, 16), False, k == 15)

        renew(0)
        tt(A("TM"), PB(b, 0, 256), A("BD2"), OP.mult)
        b = nb()
        mm(PB(b, 0, 128), A("TM", 0, 128), A("AB", 0, 128))
        mm(PB(b, 128, 256), A("TM", 128, 256), A("AB", 128, 256))
        mm(PB(b, 256, 384), A("TM", 0, 128), A("AB", 128, 256))
        b2 = nb()
        mm(PB(b2, 0, 256), A("IDB"), A("R2"), True, first)
        if not first:
            mm(PB(b2, 0, 256), A("NID"), A("R1"), False, True)
        act(A("NN"), PB(b2, 0, 256), FN.Relu, scale=1.0 / 8192)
        dist(0)
        tt(A("RB", 0, 256), PB(b, 0, 256), A("AB", 256, 512), OP.mult)
        tt(A("RB", 256, 384), PB(b, 256, 384), A("AB", 384, 512), OP.mult)
        b = conv("RB", 0, 384)
        tt(A("AC"), PB(b, 0, 16), A("WO2"), OP.is_lt)
        ts(A("AT2", 0, 8), PB(b, 16, 24), 0.0, OP.is_equal)
        tt(A("AC", 8, 16), A("AC", 8, 16), A("AT2", 0, 8), OP.mult)
        tt(A("ACT"), A("AC"), A("AL"), OP.mult)
        tt(A("ATH"), A("ACT"), A("CO"), OP.min)
        expand(bc := nb(), "ATH", 16)
        tt(A("OLI"), A("ALV"), A("AC"), OP.mult)
        tt(A("OLI"), A("OLI"), A("DUM"), OP.add)
        cp(A("OL16"), A("OLI"))
        b2 = nb()
        mm(PB(b2, 0, 256), A("SP"), A("NN"))
        ts(A("CT", 0, 256), PB(b2, 0, 256), kc(1), OP.mult, 0.0, OP.max)
        if not end:
            act(A("KLB"), PB(b2, 0, 256), FN.Relu)
        dist(1)
        oc = "OC%d" % ((r + s) % 2)
        cp(("I", A(oc), A("OL16")), A("OV"))
        act(A("OG", 0, 256), ("I", A(oc), A("C16")), FN.Copy)
        if not end:
            act(A("OG", 256, 512), ("I", A(oc), VL16), FN.Copy)
        if not final:
            iota(A(oc), [[0, 1792]], 0, 0)
        if not end:
            bo = conv("OG", 0, 512)
        tt(PB(bc, 0, 256), PB(bc, 0, 256), A("OG", 0, 256), OP.is_gt)
        tt(A("LF1"), A("ACT"), A("ATH"), OP.subtract)
        act(A("NAQ"), A("ATH"), FN.Identity, scale=100.0, bias=-1.0)
        tt(A("NAQ"), A("NAQ"), NA_, OP.min)
        act(A("ZE"), A("ATH"), FN.Identity, bias=-1.0)
        if not end:
            act(A("LAB"), PB(bo, 0, 32), FN.Identity, scale=0.0625, bias=-1.0)
            tt(A("LCX"), A("LAB", 0, 16), A("LAB", 16, 32), OP.subtract)
        tt(A("QKM"), PB(bc, 0, 256), A("QG"), OP.mult)
        dist(2)
        if not end:
            bm = nb()
            mm(PB(bm, 0, 256), A("IDB"), A("KLB"))
            tt(A("CT", 512, 768), PB(bm, 0, 256), A("QR"), OP.mult)
        if not final:
            act(A("NDD", 256, 512), ("I", A("BB", 0, nodes), A("C16")), FN.Copy)
            if not end:
                ts(A("CT", 256, 512), A("NDD", 256, 512), 0.0625, OP.mult)
        dist(3)
        bb = conv("CT", 0, 256 if end else 768)
        tt(A("DF", 32, 48), PB(bb, 0, 16), NA_, OP.subtract)
        ts(A("FUL"), PB(bb, 0, 16), 0.0, OP.is_equal)
        if not end:
            ts(A("BX1"), PB(bb, 16, 32), 512.0, OP.is_ge, 7680.0, OP.mult)
            if nodes > 1024:
                ts(A("BX2"), PB(bb, 16, 32), 1024.0, OP.is_ge, 8192.0, OP.mult)
                tt(A("BX1"), A("BX1"), A("BX2"), OP.add)
            tt(A("BX1"), A("BX1"), AD_, OP.subtract)
            tt(A("BX1"), PB(bb, 16, 32), A("BX1"), OP.add)
            tt(A("DF", 16, 32), PB(bb, 32, 48), A("BX1"), OP.add)
            tt(A("DF", 0, 16), A("CO"), V_, OP.subtract)
        tt(A("ADD"), AD_, A("D12", 0, 16), OP.subtract)
        tt(A("CND", 0, 16), A("CO"), A("DUM"), OP.subtract)
        ts(A("ES"), A("E16"), -2048.0, OP.add)
        renew(1)
        mm(PB(1, 0, 256), A("LW2"), A("NN"), True, False)
        mm(PB(1, 0, 256), A("SPH"), A("ONE"), False, False)
        act(A("FG"), PB(0, 0, 256), FN.Sign, bias=kc(7))
        mm(PB(1, 0, 256), A("SPH"), A("FG"), False, True)
        bh = nb()
        OH = PB(bh, 0, 256)
        act(OH, PB(1, 0, 256), FN.Relu)
        tt(A("M3", 0, 256), OH, A("QKM"), OP.mult)
        tt(A("M3", 256, 512), OH, A("ES"), OP.mult)
        ts(A("M3", 512, 768), OH, kc(1), OP.mult)
        ts(A("OHC"), A("M3", 0, 256), 0.0, OP.not_equal)
        bk = nb()
        for h in range(2):
            mm(PB(bk, 8 * h, 8 * h + 8), A("M3", 128 * h, 128 * h + 128), A("GSEL"))
        act(A("KP"), PB(bk, 0, 16), FN.Copy)
        act(A("KPN"), PB(bk, 0, 16), FN.Copy, scale=-1.0)
        po = conv("M3", 0, 768)
        MQ, ML, KL = PB(po, 0, 16), PB(po, 16, 32), PB(po, 32, 48)
        ts(A("LDQ"), MQ, 0.0, OP.is_gt, -2048.0, OP.add)
        ts(A("LQ", 0, 16), ML, 2048.0, OP.add)
        tt(A("LQ", 16, 32), MQ, A("LDQ"), OP.subtract)
        cp(A("LU"), A("LQ"))
        CC, CC2, TWO, LF = A("FTB", 0, 16), A("FTB", 0, 32), A("FTB", 32, 48), A("FTB", 48, 64)
        ts(CC, MQ, 0.0, OP.not_equal)
        ts(A("FTB", 16, 32), MQ, 0.0, OP.not_equal)
        tt(A("LF2"), KL, A("NAQ"), OP.is_equal)
        tt(A("DN"), KL, A("ZE"), OP.is_equal)
        act(A("XQ"), ("I", A("X", 0, 4096), A("LU", 16, 32)), FN.Copy)
        act(A("XL"), ("I", A("X", 0, 4096), A("LU", 0, 16)), FN.Copy)
        bx = nb()
        mm(PB(bx, 0, 256), A("GEI"), A("OHC"))
        mm(PB(bx, 256, 512), A("IDB"), A("ONE"), True, False)
        mm(PB(bx, 256, 512), A("GEN"), A("OHC"), False, True)
        for gp in (3, 2, 0, 1) if EQS == 2 else (3, 0, 1, 2):
            bq = nb()
            for z in range(2):
                q = 2 * gp + z
                mm(PB(bq, 256 * z, 256 * z + 256), A("GB", 128 * q, 128 * q + 128), A("M3", 0, 256))
            for z in range(2):
                q = 2 * gp + z
                h0, h1 = PB(bq, 256 * z, 256 * z + 256), PB(bq, 256 * z + 128, 256 * z + 256)
                if gp >= 4 - EQS:
                    o = 384 * (q - 4)
                    act(A("AEQ", o, o + 256), h0, FN.Abs, bias=A("KPN", q, q + 1))
                    act(A("AEQ", o + 256, o + 384), h1, FN.Abs, bias=A("KPN", 8 + q, 9 + q))
                else:
                    ts(A("EQ", 384 * q, 384 * q + 256), h0, A("KP", q, q + 1), OP.is_equal)
                    ts(A("EQ", 384 * q + 256, 384 * q + 384), h1, A("KP", 8 + q, 9 + q), OP.is_equal)
        renew(0, 1)
        e0 = 768 * (2 - EQS)
        act(A("EQ", 1536 + e0, 3072), A("AEQ", e0, 1536), FN.Relu, scale=-1.0, bias=1.0)
        for q in range(8):
            W, B_ = A("W0", 112 - 16 * q, 240 - 16 * q), A("BIG", 112 - 16 * q, 240 - 16 * q)
            mm(PB(0, 0, 128), W, A("EQ", 384 * q, 384 * q + 128), q == 0, q == 7)
            mm(PB(1, 0, 128), B_, A("EQ", 384 * q + 128, 384 * q + 256), q == 0, False)
            mm(PB(1, 0, 128), W, A("EQ", 384 * q + 256, 384 * q + 384), False, q == 7)
        tt(LF, A("LF2"), A("LF1"), OP.add)
        ts(A("RW"), A("LQ"), 15, OP.bitwise_and)
        tt(A("TW0"), A("RW", 0, 16), A("RW", 16, 32), OP.not_equal)
        tt(TWO, A("TW0"), CC, OP.mult)
        bsum = nb()
        mm(PB(bsum, 0, 256), A("IDB"), A("XQ"), True, False)
        mm(PB(bsum, 0, 256), A("IDB"), A("XL"), False, True)
        tt(A("FL", 0, 128), PB(0, 0, 128), A("WB2"), OP.is_lt)
        tt(A("FL", 128, 256), PB(1, 0, 128), A("WB2"), OP.is_lt)
        bf = conv("FL", 0, 256)
        ts(A("XB"), PB(bsum, 0, 256), 0.5, OP.mult, -0.25, OP.add)
        tt(A("XS"), A("LQ", 16, 32), A("DX"), OP.subtract)
        ts(A("XF"), MQ, 0.0, OP.not_equal, 0.0625, OP.mult)
        tt(A("XS"), A("XS"), A("XF"), OP.mult)
        tt(A("XS"), PB(bf, 0, 16), A("XS"), OP.mult)
        tt(A("XS"), A("XS"), A("DX"), OP.add)
        cp(A("XSU"), A("XS"))
        cp(("I", A("X"), A("XSU")), A("XB"))
        if not end:
            for c in range(4):
                queries(c)
        tt(A("Q3", 32, 48), A("DF", 32, 48), A("DN"), OP.mult)
        if not end:
            tt(A("Q3", 16, 32), A("DF", 16, 32), A("DN"), OP.mult)
            tt(A("Q3", 0, 16), A("DF", 0, 16), A("DN"), OP.mult)
        adl = AD_
        if not final:
            ts(A("RWF"), A("RW"), 512.0, OP.mult)
            tt(A("RWF"), A("RWF"), A("NBD"), OP.add)
            tt(A("A12"), A("RWF"), A("FTB", 16, 48), OP.mult)
            tt(A("A12"), A("A12"), A("D12"), OP.add)
            tt(A("LDL"), LF, A("ADD"), OP.mult)
            tt(A("A12", 0, 16), A("A12", 0, 16), A("LDL"), OP.add)
            cp(A("A12U"), A("A12"))
            cp(("I", A("CF", 0, 16896 if r == 0 else CFW), A("A12U")), A("ND"))
        if end:
            tt(NA_, NA_, A("Q3", 32, 48), OP.add)
            act(A("NAH"), NA_, FN.Copy)
        else:
            tt(A("ST"), A("ST"), A("Q3"), OP.add)
            cp(A("VA16"), A("ST", 0, 32))
            act(A("NAH"), NA_, FN.Copy)
            tt(A("VMD"), V_, A("DUM"), OP.subtract)
            tt(A("SV"), A("DN"), A("FUL"), OP.mult)
            ba = nb()
            mm(PB(ba, 0, 16), A("IDB"), A("AL"), True, False)
            mm(PB(ba, 0, 16), A("NID"), CC, False, False)
            mm(PB(ba, 0, 16), A("NID"), LF, False, False)
            mm(PB(ba, 0, 16), A("NID"), A("SV"), False, True)
            act(A("AL"), PB(ba, 0, 16), FN.Copy)
            tt(A("ALV"), PB(ba, 0, 16), A("VMD"), OP.mult)
            act(A("AL5"), PB(ba, 0, 16), FN.Identity, scale=512.0, bias=-1.0)
            tt(A("KX"), A("LCX"), A("DN"), OP.mult)
            tt(A("KX"), A("KX"), A("LAB", 16, 32), OP.add)
            tt(A("KXI"), A("KX"), A("AL5"), OP.min)
            digits()
        tt(A("CL"), A("CND"), CC2, OP.mult)
        tt(A("CL"), A("CL"), A("DCN"), OP.add)
        cp(A("CLU"), A("CL"))
        tt(A("T1"), PB(bx, 0, 256), A("EZ"), OP.mult)
        tt(A("T3"), PB(bx, 0, 256), A("QZ"), OP.mult)
        tt(A("FR"), PB(bx, 256, 512), A("EZ"), OP.mult)
        be = nb()
        for q in range(16):
            mm(PB(be, q, 512, 16), SELR(q), A("FTB", 32, 64))
        even, odd = A("LZ", nbase, nbase + 512, 2), A("LZ", nbase + 1, nbase + 512, 2)
        tt(PB(be, 256, 512), PB(be, 256, 512), A(qza), OP.mult)
        if first:
            tt(odd, PB(be, 0, 256), A("T3"), OP.mult)
            tt(even, PB(be, 256, 512), A("T1"), OP.add)
        else:
            tt(PB(be, 0, 256), PB(be, 0, 256), A("T3"), OP.mult)
            tt(odd, PB(be, 0, 256), odd, OP.add)
            tt(PB(be, 256, 512), PB(be, 256, 512), A("T1"), OP.add)
            tt(even, PB(be, 256, 512), even, OP.add)
        cp(("I", A("LZ"), A("CLU", 0, 16)), A("FR"))
        if not final:
            cp(("I", A("BB"), A("CLU")), A("NDD"))

    def travel(r):
        renew(2)
        expand(2, "NAH", 16)
        ts(A("OHA"), PB(2, 0, 256), kc(1), OP.is_equal)
        b = nb()
        mm(PB(b, 0, 256), A("GEI"), A("OHA"))
        tt(PB(b, 0, 256), PB(b, 0, 256), A("HD"), OP.mult)
        tt(PB(b, 0, 256), PB(b, 0, 256), A("QI"), OP.add)
        lo = 256 * r
        qx = A("QX", lo, lo + 256)
        cp(qx, PB(b, 0, 256))
        cp(A("QN", lo, lo + 32), A("QX", lo, lo + 32))
        tr, free = [], {}
        dsts = [(e, T.cores[(rank + e) % N]) for e in range(1, N)]
        used = []
        for e, d in sorted(dsts, key=lambda x: len(topo.engines(core, x[1]))):
            es = [x for x in topo.engines(core, d) if x not in used][:2]
            used += es
            rid, pid, se = topo.addr(d)
            c0 = lo + 32 * e
            tr.append(RemoteDMATransfer(dst_ids=[DstId(rid=rid, pnc=pid)], dma_engine_mask=sum(1 << x for x in es),
                                        remote_sem=T.sem["arr%d" % r], src=T.QX[:, c0:c0 + 32], dst=T.QN[:, c0:c0 + 32], alu_op=0))
        do("G", lambda e: e.remote_dma_fused(tr, local_sem=T.sem["loc"]), [A("QN", lo + 32, lo + 256)], [qx],
           sem="arr%d" % r, inc=len(used), cost=(1500.0, 0, 0, 0, 0, 0), lat=5000.0)

    for s in range(3):
        step(0, s)
    travel(0)
    iota(A("ND", 0, 256), [[2, 256]], 1024, 0)
    iota(A("ND", 256, 512), [[2, 256]], 1025, 0)
    requests(1)
    digits()
    cp(A("RWF", 0, 16), A("LQ", 16, 32))
    cp(A("BG"), ("I", A("BB", 0, 1024), VL16))
    b = conv("BG", 0, 256)
    ts(A("BX1"), PB(b, 0, 16), 8192.0, OP.is_ge, 7680.0, OP.mult)
    ts(A("LDB"), PB(b, 0, 16), 0.0625, OP.mult)
    tt(A("LDB"), A("LDB"), A("BX1"), OP.add)
    ts(A("RWF", 0, 16), A("RWF", 0, 16), 512.0, OP.mult)
    tt(A("ST", 16, 32), A("LDB"), A("RWF", 0, 16), OP.add)
    cp(AD16, A("ST", 16, 32))
    for c in range(4):
        queries(c)
    requests2(1)
    hashes(1)
    for s in range(3):
        step(1, s)
    travel(1)
    store("Y", "yd", T.yd[:, :], A("X", 0, 4096))
    act(A("LZ", 0, 768), A("LZ", 0, 768), FN.Identity, scale=-1.0, bias=4095.0)
    store("Y", "ye0", T.ye[:, 0:768], A("LZ", 0, 768))
    ts(A("LZ", 768, 1536), A("LZ", 768, 1536), -1.0, OP.mult, 4095.0, OP.add)
    store("Y", "ye1", T.ye[:, 768:1536], A("LZ", 768, 1536))
    cp(A("YR"), A("QN", 256, 512))
    store("Y", "yr", T.yr[:, :], A("YR"))
    if not _ORDER:
        _ORDER.append(order())
    for i in _ORDER[0][0]:
        issue(*nodes[i][:6])
    for sname in sorted(cnt):
        need("G", sname, cnt[sname])
